import numpy as np
import ml_dtypes


def mxq(x, axis, fmt="e4m3"):
    dtype, down = {"e4m3": (ml_dtypes.float8_e4m3fn, 7), "e5m2": (ml_dtypes.float8_e5m2, 14)}[fmt]
    v = np.moveaxis(np.asarray(x, np.float32).astype(ml_dtypes.bfloat16).astype(np.float64), axis, -1)
    blocks = v.reshape(v.shape[:-1] + (-1, 32))
    amax = np.abs(blocks).max(-1, keepdims=True)
    byte = np.maximum(np.where(amax > 0, np.frexp(amax)[1] - 1 + 127, 0) - down, 1)
    scale = np.exp2(byte - 127.0)
    codes = (blocks / scale).astype(np.float32).astype(dtype).astype(np.float64)
    return np.moveaxis((codes * scale).reshape(v.shape), -1, axis)


WIDE = False


def mx_kscale(k):
    if not WIDE:
        return np.ones(k)
    levels = np.array([10, -10, 5, -5, 0])
    if k % 512:
        return np.exp2(np.random.permutation(np.resize(levels, k // 32))).repeat(32)
    a = np.empty((k // 512, 16))
    for p in range(k // 512):
        a[p, :8] = np.random.permutation(np.resize(levels, 8))
        for g in range(8):
            far = levels[np.abs(levels - a[p, g]) >= 10]
            a[p, g + 8] = far[np.random.randint(len(far))]
    return np.exp2(a.ravel()).repeat(32)


def f64(x):
    return np.asarray(x).astype(np.float64)


def striped(idx):
    return np.tile(idx.reshape(-1, 16).T, (8, 1)).astype(np.uint16)


def unstriped(offs):
    return offs[:16].T.reshape(-1).astype(np.int64)


E2M1 = np.array([0.0, 0.5, 1.0, 1.5, 2.0, 3.0, 4.0, 6.0, -0.0, -0.5, -1.0, -1.5, -2.0, -3.0, -4.0, -6.0])


def pack_weight(w, fmt):
    k, n = w.shape
    w = f64(np.asarray(w, np.float32).astype(ml_dtypes.bfloat16)).reshape(k // 32, 32, n)
    amax = np.abs(w).max(1)
    if fmt == "e4m3":
        byte = np.frexp(amax)[1] - 1 + 127 - 7
    else:
        mant, ex = np.frexp(amax / 6.0)
        byte = np.where(mant > 0.5, ex, ex - 1) + 127
    byte = np.clip(np.where(amax > 0, byte, 1), 1, 254)
    scaled = (w * np.exp2(127.0 - byte)[:, None, :]).reshape(k, n).astype(np.float32)
    by_word = np.ascontiguousarray(scaled.reshape(k // 512, 128, 4, n).transpose(0, 1, 3, 2))
    if fmt == "e4m3":
        words = by_word.astype(ml_dtypes.float8_e4m3fn).view(np.uint8)
    else:
        c = by_word.astype(ml_dtypes.float4_e2m1fn).view(np.uint8) & 0xF
        words = (c[..., 0::2] | (c[..., 1::2] << 4)).reshape(k // 512, 128, 2 * n)
    return np.ascontiguousarray(words), np.ascontiguousarray(byte.astype(np.uint8).reshape(k // 512, 16, n))


def unpack_weight(words, scales, fmt):
    g, _, n = scales.shape
    words = np.ascontiguousarray(words).reshape(g, 128, n, -1)
    if fmt == "e4m3":
        vals = words.view(ml_dtypes.float8_e4m3fn).astype(np.float64)
    else:
        nib = np.empty((g, 128, n, 4), np.uint8)
        nib[..., 0::2] = words & 0xF
        nib[..., 1::2] = words >> 4
        vals = E2M1[nib]
    vals = vals * np.repeat(np.exp2(scales.astype(np.float64) - 127.0), 8, axis=1)[..., None]
    return vals.transpose(0, 1, 3, 2).reshape(g * 512, n)


def sigmoid(v):
    return 1.0 / (1.0 + np.exp(-np.maximum(v, -700.0)))


K, T, E, C, H, N, HOT = 1536, 768, 6, 128, 512, 256, 1


def by_expert(wq, xq):
    return np.concatenate([wq[e].T @ xq[:, e * C:(e + 1) * C] for e in range(E)], axis=1)


def setup_inputs():
    n = np.random.standard_normal
    s = mx_kscale(K)
    u = mx_kscale(H)
    slot_token = np.random.permutation(T)[:E * C]
    x = pack_weight(n((K, T)) * s[:, None], "e4m3")
    w1h = [pack_weight(m, "e4m3") for m in n((HOT, K, H)) / np.sqrt(K) / s[None, :, None]]
    w3h = [pack_weight(m, "e4m3") for m in n((HOT, K, H)) / np.sqrt(K) / s[None, :, None] * u]
    w2h = [pack_weight(m, "e4m3") for m in n((HOT, H, N)) / np.sqrt(H) / u[None, :, None]]
    w1c = [pack_weight(m, "e2m1") for m in n((E - HOT, K, H)) / np.sqrt(K) / s[None, :, None]]
    w3c = [pack_weight(m, "e2m1") for m in n((E - HOT, K, H)) / np.sqrt(K) / s[None, :, None] * u]
    w2c = [pack_weight(m, "e2m1") for m in n((E - HOT, H, N)) / np.sqrt(H) / u[None, :, None]]
    return {
        "x_words": x[0],
        "x_scales": x[1],
        "w1h_words": np.stack([m[0] for m in w1h]),
        "w1h_scales": np.stack([m[1] for m in w1h]),
        "w3h_words": np.stack([m[0] for m in w3h]),
        "w3h_scales": np.stack([m[1] for m in w3h]),
        "w2h_words": np.stack([m[0] for m in w2h]),
        "w2h_scales": np.stack([m[1] for m in w2h]),
        "w1c_words": np.stack([m[0] for m in w1c]),
        "w1c_scales": np.stack([m[1] for m in w1c]),
        "w3c_words": np.stack([m[0] for m in w3c]),
        "w3c_scales": np.stack([m[1] for m in w3c]),
        "w2c_words": np.stack([m[0] for m in w2c]),
        "w2c_scales": np.stack([m[1] for m in w2c]),
        "gate": np.tile(np.random.uniform(0.2, 1.0, E * C), (128, 1)).astype(np.float32),
        "offs": striped(slot_token),
    }


def reference(x_words, x_scales, w1h_words, w1h_scales, w3h_words, w3h_scales, w2h_words, w2h_scales, w1c_words, w1c_scales, w3c_words, w3c_scales, w2c_words, w2c_scales, gate, offs):
    w1h = np.stack([unpack_weight(w1h_words[e], w1h_scales[e], "e4m3") for e in range(HOT)])
    w3h = np.stack([unpack_weight(w3h_words[e], w3h_scales[e], "e4m3") for e in range(HOT)])
    w2h = np.stack([unpack_weight(w2h_words[e], w2h_scales[e], "e4m3") for e in range(HOT)])
    w1c = np.stack([unpack_weight(w1c_words[e], w1c_scales[e], "e2m1") for e in range(E - HOT)])
    w3c = np.stack([unpack_weight(w3c_words[e], w3c_scales[e], "e2m1") for e in range(E - HOT)])
    w2c = np.stack([unpack_weight(w2c_words[e], w2c_scales[e], "e2m1") for e in range(E - HOT)])
    idx = unstriped(offs)
    xq = unpack_weight(x_words, x_scales, "e4m3")[:, idx]
    w1 = [*w1h, *w1c]
    w3 = [*w3h, *w3c]
    w2 = [*w2h, *w2c]
    h = sigmoid(by_expert(w1, xq)) * by_expert(w3, xq)
    y = by_expert(w2, mxq(h, 0, "e4m3"))
    out = np.zeros((N, T))
    out[:, idx] = f64(gate[:1]) * y
    return out

@@ -1,0 +1,177 @@
+from contextlib import ExitStack
+
+import concourse.mybir as mybir
+from concourse.masks import make_identity
+
+K, T, E, C, H, N = 1536, 768, 6, 128, 512, 256
+FLOPS = 2 * E * C * (2 * K * H + H * N)
+
+F32 = mybir.dt.float32
+BF16 = mybir.dt.bfloat16
+I32 = mybir.dt.int32
+U32 = mybir.dt.uint32
+U16 = mybir.dt.uint16
+U8 = mybir.dt.uint8
+FP8X4 = mybir.dt.float8_e4m3fn_x4
+FP4X4 = mybir.dt.float4_e2m1fn_x4
+MULT = mybir.AluOpType.mult
+SIGMOID = mybir.ActivationFunctionType.Sigmoid
+
+P = 128
+S = K // 512
+COLD = E - 1
+
+
+def tile_moe_hot_glu_sigmoid_kernel(
+    tc, x_words, x_scales, w1h_words, w1h_scales, w3h_words, w3h_scales, w2h_words, w2h_scales,
+    w1c_words, w1c_scales, w3c_words, w3c_scales, w2c_words, w2c_scales, gate, offs, out,
+):
+    nc = tc.nc
+    with ExitStack() as ctx:
+        keep = ctx.enter_context(tc.tile_pool(name="keep", bufs=1))
+        work = ctx.enter_context(tc.tile_pool(name="work", bufs=3))
+        psum = ctx.enter_context(tc.psum_pool(name="psum", bufs=2))
+
+        offsets = keep.tile([P, T // 16], U16, name="offsets")
+        nc.sync.dma_start(offsets[:], offs)
+
+        xw_in = [keep.tile([P, T], I32, name="xw_in%d" % s, align_bytes=64) for s in range(S)]
+        xs_in = keep.tile([P, S, T], U8, name="xs_in", align_bytes=64)
+        sc1 = keep.tile([P, COLD * S, H], U8, name="sc1", align_bytes=64)
+        sc3 = keep.tile([P, COLD * S, H], U8, name="sc3", align_bytes=64)
+        sc2 = keep.tile([P, COLD, N], U8, name="sc2", align_bytes=64)
+        for plane in (xs_in, sc1, sc3, sc2):
+            nc.vector.memset(plane[:].bitcast(I32), 0)
+
+        def scale_rows(plane, row0, dram):
+            rows = dram.bitcast(I32).rearrange("g (q r) w -> r q g w", r=4)
+            return [(plane.bitcast(I32)[row0 + r : P : 32], rows[r]) for r in range(4)]
+
+        for s in range(S):
+            nc.sync.dma_start(xw_in[s][:], x_words[s].rearrange("p t d -> p (t d)").bitcast(I32))
+        for pair in scale_rows(xs_in[:], 0, x_scales):
+            nc.scalar.dma_start(*pair)
+        for pair in scale_rows(sc1[:], 0, w1c_scales.rearrange("f s b i -> (f s) b i")):
+            nc.gpsimd.dma_start(*pair)
+        for pair in scale_rows(sc3[:], 0, w3c_scales.rearrange("f s b i -> (f s) b i")):
+            nc.scalar.dma_start(*pair)
+        for pair in scale_rows(sc2[:], 0, w2c_scales.rearrange("f s b i -> (f s) b i")):
+            nc.gpsimd.dma_start(*pair)
+
+        ident = keep.tile([P, P], F32, name="ident")
+        make_identity(nc, ident[:])
+
+        w1 = [keep.tile([P, S, (4 if e == 0 else 2) * H], U8, name="w1_%d" % e, align_bytes=64) for e in range(E)]
+        w3 = [keep.tile([P, S, (4 if e == 0 else 2) * H], U8, name="w3_%d" % e, align_bytes=64) for e in range(E)]
+        w2h = keep.tile([P, 4 * N], U8, name="w2h", align_bytes=64)
+        w2a = keep.tile([P, 3, 2 * N], U8, name="w2a", align_bytes=64)
+        w2b = keep.tile([P, 2, 2 * N], U8, name="w2b", align_bytes=64)
+        gate_sb = keep.tile([P, T], F32, name="gate_sb")
+
+        last = (COLD - 1) * S
+        small = (scale_rows(sc1[:, last : last + S, :], 4, w1h_scales[0])
+                 + scale_rows(sc3[:, last : last + S, :], 8, w3h_scales[0])
+                 + scale_rows(sc2[:, COLD - 1 : COLD, :], 12, w2h_scales[0]))
+        w2c = w2c_words.bitcast(I32).rearrange("f s p w -> p (f s) w")
+        big = []
+        for e in range(1, E):
+            big.append((w1[e][:].bitcast(I32), w1c_words[e - 1].bitcast(I32).rearrange("s p w -> p s w")))
+            big.append((w3[e][:].bitcast(I32), w3c_words[e - 1].bitcast(I32).rearrange("s p w -> p s w")))
+            if e == 2:
+                big.append((w2a[:].bitcast(I32), w2c[:, 0:3, :]))
+            if e == 3:
+                big.append((gate_sb[:, 128:512], gate[:, 128:512]))
+        big.append((w2b[:].bitcast(I32), w2c[:, 3:5, :]))
+        big.append((gate_sb[:, 512:768], gate[:, 512:768]))
+        big.append((w1[0][:].bitcast(I32), w1h_words[0].rearrange("s p i d -> p s (i d)").bitcast(I32)))
+        for s in range(S):
+            big.append((w3[0][:, s, :].bitcast(I32), w3h_words[0, s].rearrange("p i d -> p (i d)").bitcast(I32)))
+        big.append((w2h[:].bitcast(I32), w2h_words[0, 0].rearrange("p i d -> p (i d)").bitcast(I32)))
+        big.append((gate_sb[:, 0:128], gate[:, 0:128]))
+        for j, pair in enumerate(big):
+            nc.sync.dma_start(*pair)
+            if j < len(small):
+                nc.sync.dma_start(*small[j])
+
+        groups = [(128, 256), (256, 512), (512, 768), (0, 128)]
+        gathered = {}
+
+        def gather(a, b):
+            words = keep.tile([P, S, b - a], U32, name="xw_%d" % max(a, C), align_bytes=64)
+            scales = keep.tile([P, S, b - a], U8, name="xs_%d" % max(a, C), align_bytes=64)
+            sl = offsets[:, a // 16 : b // 16]
+            for s in range(S):
+                nc.vector.tensor_copy(words[:, s, :], xw_in[s][:].bitcast(U32).indirect(sl))
+            for s in range(S):
+                nc.vector.tensor_copy(scales[:, s, :], xs_in[:, s, :].indirect(sl))
+            for e in range(a // C, b // C):
+                gathered[e] = (words, scales, slice(e * C - a, (e + 1) * C - a))
+
+        windows = [keep.tile([P, T], F32, name="window%d" % h) for h in range(2)]
+
+        def first_layer(e):
+            words, scales, cols = gathered[e]
+            banks = []
+            for w, sc, row0, tag in ((w1, sc1, 4, "a"), (w3, sc3, 8, "b")):
+                acc = psum.tile([P, H], F32, name=tag)
+                for s in range(S):
+                    if e == 0:
+                        rhs, rs = w[e][:, s, :].bitcast(FP8X4), sc[row0:P, last + s, :]
+                    else:
+                        rhs, rs = w[e][:, s, :].bitcast(FP4X4), sc[:, (e - 1) * S + s, :]
+                    nc.tensor.matmul_mx(acc[:], lhsT=words[:, s, cols].bitcast(FP8X4), lhsT_scale=scales[:, s, cols],
+                                        rhs=rhs, rhs_scale=rs, start=(s == 0), stop=(s == S - 1))
+                banks.append(acc)
+            sg = work.tile([P, 2, P, 2], F32, name="sg")
+            nc.scalar.activation(sg[:], banks[0][:].rearrange("c (p u j) -> c u p j", u=2, j=2), SIGMOID)
+            hid = work.tile([P, 2, P, 2], BF16, name="hid", align_bytes=64)
+            nc.vector.tensor_tensor(hid[:], banks[1][:].rearrange("c (p u j) -> c u p j", u=2, j=2), sg[:], MULT)
+            return hid
+
+        def turn(hid):
+            pairs = hid[:].rearrange("c u p j -> c (u p j)").bitcast(F32)
+            turned = psum.tile([P, 2, C], F32, name="turned")
+            for u in range(2):
+                nc.tensor.transpose(turned[:, u, :], pairs[:, u * P : (u + 1) * P], ident[:])
+            grouped = work.tile([P, C * 4], BF16, name="grouped", align_bytes=64)
+            nc.scalar.copy(grouped[:].bitcast(F32).rearrange("p (c u) -> p c u", u=2), turned[:].rearrange("p u c -> p c u"))
+            hq = work.tile([P, C], U32, name="hq", align_bytes=64)
+            hs = work.tile([P, C], U8, name="hs", align_bytes=64)
+            nc.vector.quantize_mx(hq[:].bitcast(FP8X4), hs[:], grouped[:])
+            return hq, hs
+
+        def second_layer(e, hq, hs):
+            y = psum.tile([P, 2, C], F32, name="y")
+            for h in range(2):
+                cols = slice(h * P, (h + 1) * P)
+                if e == 0:
+                    lhsT, ls = w2h[:, h * 4 * P : (h + 1) * 4 * P].bitcast(FP8X4), sc2[12:P, COLD - 1, cols]
+                else:
+                    src = w2a[:, e - 1, :] if e <= 3 else w2b[:, e - 4, :]
+                    lhsT, ls = src[:, h * 2 * P : (h + 1) * 2 * P].bitcast(FP4X4), sc2[:, e - 1, cols]
+                nc.tensor.matmul_mx(y[:, h, :], lhsT=lhsT, lhsT_scale=ls, rhs=hq[:].bitcast(FP8X4), rhs_scale=hs[:],
+                                    start=True, stop=True)
+            ysb = work.tile([P, 2, C], F32, name="ysb")
+            nc.scalar.copy(ysb[:], y[:])
+            return ysb
+
+        def scatter(e, ysb):
+            sl = offsets[:, e * C // 16 : (e + 1) * C // 16]
+            for h in range(2):
+                nc.vector.tensor_tensor(windows[h][:].indirect(sl), ysb[:, h, :], gate_sb[:, e * C : (e + 1) * C], MULT)
+
+        for group in groups[:3]:
+            gather(*group)
+        order = [1, 2, 3, 4, 5, 0]
+        hids, codes = {}, {}
+        for step in range(len(order) + 2):
+            if step < len(order):
+                hids[step] = first_layer(order[step])
+            if 1 <= step <= len(order):
+                codes[step - 1] = turn(hids[step - 1])
+            if step >= 2:
+                scatter(order[step - 2], second_layer(order[step - 2], *codes[step - 2]))
+            if step == 0:
+                gather(*groups[3])
+        for h in range(2):
+            nc.sync.dma_start(out[h * P : (h + 1) * P, :], windows[h][:])

@@ -30,7 +30,7 @@ def tile_moe_hot_glu_sigmoid_kernel(
     with ExitStack() as ctx:
         keep = ctx.enter_context(tc.tile_pool(name="keep", bufs=1))
         work = ctx.enter_context(tc.tile_pool(name="work", bufs=3))
-        psum = ctx.enter_context(tc.psum_pool(name="psum", bufs=2))
+        psum = ctx.enter_context(tc.psum_pool(name="psum", bufs=1))
 
         offsets = keep.tile([P, T // 16], U16, name="offsets")
         nc.sync.dma_start(offsets[:], offs)
@@ -40,7 +40,10 @@ def tile_moe_hot_glu_sigmoid_kernel(
         sc1 = keep.tile([P, COLD * S, H], U8, name="sc1", align_bytes=64)
         sc3 = keep.tile([P, COLD * S, H], U8, name="sc3", align_bytes=64)
         sc2 = keep.tile([P, COLD, N], U8, name="sc2", align_bytes=64)
-        for plane in (xs_in, sc1, sc3, sc2):
+        sh1 = keep.tile([P, S, H], U8, name="sh1", align_bytes=64)
+        sh3 = keep.tile([P, S, H], U8, name="sh3", align_bytes=64)
+        sh2 = keep.tile([P, 1, N], U8, name="sh2", align_bytes=64)
+        for plane in (xs_in, sc1, sc3, sc2, sh1, sh3, sh2):
             nc.vector.memset(plane[:].bitcast(I32), 0)
 
         def scale_rows(plane, row0, dram):
@@ -49,49 +52,50 @@ def tile_moe_hot_glu_sigmoid_kernel(
 
         for s in range(S):
             nc.sync.dma_start(xw_in[s][:], x_words[s].rearrange("p t d -> p (t d)").bitcast(I32))
-        for pair in scale_rows(xs_in[:], 0, x_scales):
-            nc.scalar.dma_start(*pair)
-        for pair in scale_rows(sc1[:], 0, w1c_scales.rearrange("f s b i -> (f s) b i")):
-            nc.gpsimd.dma_start(*pair)
-        for pair in scale_rows(sc3[:], 0, w3c_scales.rearrange("f s b i -> (f s) b i")):
-            nc.scalar.dma_start(*pair)
-        for pair in scale_rows(sc2[:], 0, w2c_scales.rearrange("f s b i -> (f s) b i")):
-            nc.gpsimd.dma_start(*pair)
+        small = (scale_rows(xs_in[:], 0, x_scales)
+                 + scale_rows(sc1[:], 0, w1c_scales.rearrange("f s b i -> (f s) b i"))
+                 + scale_rows(sc3[:], 0, w3c_scales.rearrange("f s b i -> (f s) b i"))
+                 + scale_rows(sc2[:], 0, w2c_scales.rearrange("f s b i -> (f s) b i")))
+        for pair in small:
+            nc.sync.dma_start(*pair)
 
         ident = keep.tile([P, P], F32, name="ident")
         make_identity(nc, ident[:])
 
-        w1 = [keep.tile([P, S, (4 if e == 0 else 2) * H], U8, name="w1_%d" % e, align_bytes=64) for e in range(E)]
-        w3 = [keep.tile([P, S, (4 if e == 0 else 2) * H], U8, name="w3_%d" % e, align_bytes=64) for e in range(E)]
+        w1c = keep.tile([P, COLD, S, 2 * H], U8, name="w1c", align_bytes=64)
+        w3c = keep.tile([P, COLD, S, 2 * H], U8, name="w3c", align_bytes=64)
+        w2c = keep.tile([P, COLD, 2 * N], U8, name="w2c", align_bytes=64)
+        w1h = keep.tile([P, S, 4 * H], U8, name="w1h", align_bytes=64)
+        w3h = keep.tile([P, S, 4 * H], U8, name="w3h", align_bytes=64)
         w2h = keep.tile([P, 4 * N], U8, name="w2h", align_bytes=64)
-        w2a = keep.tile([P, 3, 2 * N], U8, name="w2a", align_bytes=64)
-        w2b = keep.tile([P, 2, 2 * N], U8, name="w2b", align_bytes=64)
         gate_sb = keep.tile([P, T], F32, name="gate_sb")
 
-        last = (COLD - 1) * S
-        small = (scale_rows(sc1[:, last : last + S, :], 4, w1h_scales[0])
-                 + scale_rows(sc3[:, last : last + S, :], 8, w3h_scales[0])
-                 + scale_rows(sc2[:, COLD - 1 : COLD, :], 12, w2h_scales[0]))
-        w2c = w2c_words.bitcast(I32).rearrange("f s p w -> p (f s) w")
+        def cold(tile, dram, a, b):
+            return (tile[:, a:b].rearrange("p f s w -> p (f s) w").bitcast(I32),
+                    dram[a:b].bitcast(I32).rearrange("f s p w -> p (f s) w"))
+
+        def hot(tile, dram, s):
+            return (tile[:, s, :].bitcast(I32), dram[0, s].rearrange("p i d -> p (i d)").bitcast(I32))
+
+        def second(f):
+            return (w2c[:, f, :].bitcast(I32), w2c_words[f, 0].bitcast(I32))
+
         big = []
-        for e in range(1, E):
-            big.append((w1[e][:].bitcast(I32), w1c_words[e - 1].bitcast(I32).rearrange("s p w -> p s w")))
-            big.append((w3[e][:].bitcast(I32), w3c_words[e - 1].bitcast(I32).rearrange("s p w -> p s w")))
-            if e == 2:
-                big.append((w2a[:].bitcast(I32), w2c[:, 0:3, :]))
-            if e == 3:
-                big.append((gate_sb[:, 128:512], gate[:, 128:512]))
-        big.append((w2b[:].bitcast(I32), w2c[:, 3:5, :]))
-        big.append((gate_sb[:, 512:768], gate[:, 512:768]))
-        big.append((w1[0][:].bitcast(I32), w1h_words[0].rearrange("s p i d -> p s (i d)").bitcast(I32)))
-        for s in range(S):
-            big.append((w3[0][:, s, :].bitcast(I32), w3h_words[0, s].rearrange("p i d -> p (i d)").bitcast(I32)))
-        big.append((w2h[:].bitcast(I32), w2h_words[0, 0].rearrange("p i d -> p (i d)").bitcast(I32)))
-        big.append((gate_sb[:, 0:128], gate[:, 0:128]))
-        for j, pair in enumerate(big):
+        for f in range(COLD):
+            big.append(cold(w1c, w1c_words, f, f + 1))
+            big.append(cold(w3c, w3c_words, f, f + 1))
+            if f == 1:
+                big.append((gate_sb[:, C:T], gate[:, C:T]))
+            if f >= 2:
+                big.append(second(f - 2))
+        rows1, rows3, rows2 = (scale_rows(sh1[:], 4, w1h_scales[0]), scale_rows(sh3[:], 8, w3h_scales[0]),
+                               scale_rows(sh2[:], 12, w2h_scales[0]))
+        big += rows1 + [hot(w1h, w1h_words, 0)] + rows3[:2] + [hot(w1h, w1h_words, 1)] + rows3[2:]
+        big += [hot(w1h, w1h_words, 2), hot(w3h, w3h_words, 0)] + rows2[:2] + [hot(w3h, w3h_words, 1)] + rows2[2:]
+        big += [hot(w3h, w3h_words, 2), second(COLD - 2), second(COLD - 1), (w2h[:].bitcast(I32), w2h_words[0, 0].rearrange("p i d -> p (i d)").bitcast(I32)),
+                (gate_sb[:, 0:C], gate[:, 0:C])]
+        for pair in big:
             nc.sync.dma_start(*pair)
-            if j < len(small):
-                nc.sync.dma_start(*small[j])
 
         groups = [(128, 256), (256, 512), (512, 768), (0, 128)]
         gathered = {}
@@ -109,16 +113,16 @@ def tile_moe_hot_glu_sigmoid_kernel(
 
         windows = [keep.tile([P, T], F32, name="window%d" % h) for h in range(2)]
 
-        def first_layer(e):
+        def first_layer(e, step):
             words, scales, cols = gathered[e]
             banks = []
-            for w, sc, row0, tag in ((w1, sc1, 4, "a"), (w3, sc3, 8, "b")):
-                acc = psum.tile([P, H], F32, name=tag)
+            for wh, wc, sh, sc, row0, tag in ((w1h, w1c, sh1, sc1, 4, "a"), (w3h, w3c, sh3, sc3, 8, "b")):
+                acc = psum.tile([P, H], F32, name="%s%d" % (tag, step % 2))
                 for s in range(S):
                     if e == 0:
-                        rhs, rs = w[e][:, s, :].bitcast(FP8X4), sc[row0:P, last + s, :]
+                        rhs, rs = wh[:, s, :].bitcast(FP8X4), sh[row0:P, s, :]
                     else:
-                        rhs, rs = w[e][:, s, :].bitcast(FP4X4), sc[:, (e - 1) * S + s, :]
+                        rhs, rs = wc[:, e - 1, s, :].bitcast(FP4X4), sc[:, (e - 1) * S + s, :]
                     nc.tensor.matmul_mx(acc[:], lhsT=words[:, s, cols].bitcast(FP8X4), lhsT_scale=scales[:, s, cols],
                                         rhs=rhs, rhs_scale=rs, start=(s == 0), stop=(s == S - 1))
                 banks.append(acc)
@@ -128,9 +132,9 @@ def tile_moe_hot_glu_sigmoid_kernel(
             nc.vector.tensor_tensor(hid[:], banks[1][:].rearrange("c (p u j) -> c u p j", u=2, j=2), sg[:], MULT)
             return hid
 
-        def turn(hid):
+        def turn(hid, bank):
             pairs = hid[:].rearrange("c u p j -> c (u p j)").bitcast(F32)
-            turned = psum.tile([P, 2, C], F32, name="turned")
+            turned = psum.tile([P, 2, C], F32, name=bank)
             for u in range(2):
                 nc.tensor.transpose(turned[:, u, :], pairs[:, u * P : (u + 1) * P], ident[:])
             grouped = work.tile([P, C * 4], BF16, name="grouped", align_bytes=64)
@@ -141,14 +145,13 @@ def tile_moe_hot_glu_sigmoid_kernel(
             return hq, hs
 
         def second_layer(e, hq, hs):
-            y = psum.tile([P, 2, C], F32, name="y")
+            y = psum.tile([P, 2, C], F32, name="y", bufs=2)
             for h in range(2):
                 cols = slice(h * P, (h + 1) * P)
                 if e == 0:
-                    lhsT, ls = w2h[:, h * 4 * P : (h + 1) * 4 * P].bitcast(FP8X4), sc2[12:P, COLD - 1, cols]
+                    lhsT, ls = w2h[:, h * 4 * P : (h + 1) * 4 * P].bitcast(FP8X4), sh2[12:P, 0, cols]
                 else:
-                    src = w2a[:, e - 1, :] if e <= 3 else w2b[:, e - 4, :]
-                    lhsT, ls = src[:, h * 2 * P : (h + 1) * 2 * P].bitcast(FP4X4), sc2[:, e - 1, cols]
+                    lhsT, ls = w2c[:, e - 1, h * 2 * P : (h + 1) * 2 * P].bitcast(FP4X4), sc2[:, e - 1, cols]
                 nc.tensor.matmul_mx(y[:, h, :], lhsT=lhsT, lhsT_scale=ls, rhs=hq[:].bitcast(FP8X4), rhs_scale=hs[:],
                                     start=True, stop=True)
             ysb = work.tile([P, 2, C], F32, name="ysb")
@@ -166,9 +169,9 @@ def tile_moe_hot_glu_sigmoid_kernel(
         hids, codes = {}, {}
         for step in range(len(order) + 2):
             if step < len(order):
-                hids[step] = first_layer(order[step])
+                hids[step] = first_layer(order[step], step)
             if 1 <= step <= len(order):
-                codes[step - 1] = turn(hids[step - 1])
+                codes[step - 1] = turn(hids[step - 1], "a%d" % (step % 2))
             if step >= 2:
                 scatter(order[step - 2], second_layer(order[step - 2], *codes[step - 2]))
             if step == 0:

@@ -43,8 +43,9 @@ def tile_moe_hot_glu_sigmoid_kernel(
         sh1 = keep.tile([P, S, H], U8, name="sh1", align_bytes=64)
         sh3 = keep.tile([P, S, H], U8, name="sh3", align_bytes=64)
         sh2 = keep.tile([P, 1, N], U8, name="sh2", align_bytes=64)
-        for plane in (xs_in, sc1, sc3, sc2, sh1, sh3, sh2):
-            nc.vector.memset(plane[:].bitcast(I32), 0)
+        nc.gpsimd.memset(xs_in[:].rearrange("p g w -> p (g w)").bitcast(I32), 0)
+        for plane in (sc1, sc3, sc2, sh1, sh3, sh2):
+            nc.vector.memset(plane[:].rearrange("p g w -> p (g w)").bitcast(I32), 0)
 
         def scale_rows(plane, row0, dram):
             rows = dram.bitcast(I32).rearrange("g (q r) w -> r q g w", r=4)
@@ -78,26 +79,26 @@ def tile_moe_hot_glu_sigmoid_kernel(
             return (tile[:, s, :].bitcast(I32), dram[0, s].rearrange("p i d -> p (i d)").bitcast(I32))
 
         def second(f):
-            return (w2c[:, f, :].bitcast(I32), w2c_words[f, 0].bitcast(I32))
+            cols = slice((f + 1) * C, (f + 2) * C)
+            return [(w2c[:, f, :].bitcast(I32), w2c_words[f, 0].bitcast(I32)), (gate_sb[:, cols], gate[:, cols])]
 
         big = []
         for f in range(COLD):
-            big.append(cold(w1c, w1c_words, f, f + 1))
-            big.append(cold(w3c, w3c_words, f, f + 1))
-            if f == 1:
-                big.append((gate_sb[:, C:T], gate[:, C:T]))
-            if f >= 2:
-                big.append(second(f - 2))
+            big += [cold(w1c, w1c_words, f, f + 1), cold(w3c, w3c_words, f, f + 1)]
+            if f == 0:
+                big += second(0)
+            if f >= 3:
+                big += second(f - 2)
         rows1, rows3, rows2 = (scale_rows(sh1[:], 4, w1h_scales[0]), scale_rows(sh3[:], 8, w3h_scales[0]),
                                scale_rows(sh2[:], 12, w2h_scales[0]))
         big += rows1 + [hot(w1h, w1h_words, 0)] + rows3[:2] + [hot(w1h, w1h_words, 1)] + rows3[2:]
         big += [hot(w1h, w1h_words, 2), hot(w3h, w3h_words, 0)] + rows2[:2] + [hot(w3h, w3h_words, 1)] + rows2[2:]
-        big += [hot(w3h, w3h_words, 2), second(COLD - 2), second(COLD - 1), (w2h[:].bitcast(I32), w2h_words[0, 0].rearrange("p i d -> p (i d)").bitcast(I32)),
+        big += [hot(w3h, w3h_words, 2)] + second(COLD - 2) + second(COLD - 1) + [(w2h[:].bitcast(I32), w2h_words[0, 0].rearrange("p i d -> p (i d)").bitcast(I32)),
                 (gate_sb[:, 0:C], gate[:, 0:C])]
         for pair in big:
             nc.sync.dma_start(*pair)
 
-        groups = [(128, 256), (256, 512), (512, 768), (0, 128)]
+        groups = [(128, 384), (384, 768), (0, 128)]
         gathered = {}
 
         def gather(a, b):
@@ -126,17 +127,17 @@ def tile_moe_hot_glu_sigmoid_kernel(
                     nc.tensor.matmul_mx(acc[:], lhsT=words[:, s, cols].bitcast(FP8X4), lhsT_scale=scales[:, s, cols],
                                         rhs=rhs, rhs_scale=rs, start=(s == 0), stop=(s == S - 1))
                 banks.append(acc)
-            sg = work.tile([P, 2, P, 2], F32, name="sg")
-            nc.scalar.activation(sg[:], banks[0][:].rearrange("c (p u j) -> c u p j", u=2, j=2), SIGMOID)
-            hid = work.tile([P, 2, P, 2], BF16, name="hid", align_bytes=64)
-            nc.vector.tensor_tensor(hid[:], banks[1][:].rearrange("c (p u j) -> c u p j", u=2, j=2), sg[:], MULT)
+            sg = work.tile([P, H], F32, name="sg")
+            nc.scalar.activation(sg[:], banks[0][:], SIGMOID)
+            hid = work.tile([P, H], BF16, name="hid", align_bytes=64)
+            nc.vector.tensor_tensor(hid[:], banks[1][:], sg[:], MULT)
             return hid
 
         def turn(hid, bank):
-            pairs = hid[:].rearrange("c u p j -> c (u p j)").bitcast(F32)
+            pairs = hid[:].bitcast(F32)
             turned = psum.tile([P, 2, C], F32, name=bank)
             for u in range(2):
-                nc.tensor.transpose(turned[:, u, :], pairs[:, u * P : (u + 1) * P], ident[:])
+                nc.tensor.transpose(turned[:, u, :], pairs[:, u : 2 * P : 2], ident[:])
             grouped = work.tile([P, C * 4], BF16, name="grouped", align_bytes=64)
             nc.scalar.copy(grouped[:].bitcast(F32).rearrange("p (c u) -> p c u", u=2), turned[:].rearrange("p u c -> p c u"))
             hq = work.tile([P, C], U32, name="hq", align_bytes=64)
@@ -163,7 +164,7 @@ def tile_moe_hot_glu_sigmoid_kernel(
             for h in range(2):
                 nc.vector.tensor_tensor(windows[h][:].indirect(sl), ysb[:, h, :], gate_sb[:, e * C : (e + 1) * C], MULT)
 
-        for group in groups[:3]:
+        for group in groups[:2]:
             gather(*group)
         order = [1, 2, 3, 4, 5, 0]
         hids, codes = {}, {}
@@ -174,7 +175,7 @@ def tile_moe_hot_glu_sigmoid_kernel(
                 codes[step - 1] = turn(hids[step - 1], "a%d" % (step % 2))
             if step >= 2:
                 scatter(order[step - 2], second_layer(order[step - 2], *codes[step - 2]))
-            if step == 0:
-                gather(*groups[3])
+            if step == 1:
+                gather(*groups[2])
         for h in range(2):
             nc.sync.dma_start(out[h * P : (h + 1) * P, :], windows[h][:])

@@ -20,6 +20,7 @@ SIGMOID = mybir.ActivationFunctionType.Sigmoid
 P = 128
 S = K // 512
 COLD = E - 1
+ROWS, RUN = 8, T // 8
 
 
 def tile_moe_hot_glu_sigmoid_kernel(
@@ -37,145 +38,171 @@ def tile_moe_hot_glu_sigmoid_kernel(
 
         xw_in = [keep.tile([P, T], I32, name="xw_in%d" % s, align_bytes=64) for s in range(S)]
         xs_in = keep.tile([P, S, T], U8, name="xs_in", align_bytes=64)
-        sc1 = keep.tile([P, COLD * S, H], U8, name="sc1", align_bytes=64)
-        sc3 = keep.tile([P, COLD * S, H], U8, name="sc3", align_bytes=64)
-        sc2 = keep.tile([P, COLD, N], U8, name="sc2", align_bytes=64)
-        sh1 = keep.tile([P, S, H], U8, name="sh1", align_bytes=64)
-        sh3 = keep.tile([P, S, H], U8, name="sh3", align_bytes=64)
-        sh2 = keep.tile([P, 1, N], U8, name="sh2", align_bytes=64)
+        sc1 = keep.tile([P, COLD * S, H // 4], I32, name="sc1", align_bytes=64)
+        sc3 = keep.tile([P, COLD * S, H // 4], I32, name="sc3", align_bytes=64)
+        sc2 = keep.tile([P, COLD, N // 4], I32, name="sc2", align_bytes=64)
+        hot_planes = keep.tile([P, S, H // 4], I32, name="hot_planes", align_bytes=64)
+        gate_rows = keep.tile([P, P], F32, name="gate_rows")
         nc.gpsimd.memset(xs_in[:].rearrange("p g w -> p (g w)").bitcast(I32), 0)
-        for plane in (sc1, sc3, sc2, sh1, sh3, sh2):
-            nc.vector.memset(plane[:].rearrange("p g w -> p (g w)").bitcast(I32), 0)
+        nc.gpsimd.memset(gate_rows[:], 0.0)
+        for plane in (sc1, sc3, sc2, hot_planes):
+            nc.vector.memset(plane[:].rearrange("p g w -> p (g w)"), 0)
+        sh1, sh3, sh2 = hot_planes[:], hot_planes[:], hot_planes[:, 0:1, 0 : N // 4]
 
         def scale_rows(plane, row0, dram):
             rows = dram.bitcast(I32).rearrange("g (q r) w -> r q g w", r=4)
-            return [(plane.bitcast(I32)[row0 + r : P : 32], rows[r]) for r in range(4)]
-
-        for s in range(S):
-            nc.sync.dma_start(xw_in[s][:], x_words[s].rearrange("p t d -> p (t d)").bitcast(I32))
-        small = (scale_rows(xs_in[:], 0, x_scales)
-                 + scale_rows(sc1[:], 0, w1c_scales.rearrange("f s b i -> (f s) b i"))
-                 + scale_rows(sc3[:], 0, w3c_scales.rearrange("f s b i -> (f s) b i"))
-                 + scale_rows(sc2[:], 0, w2c_scales.rearrange("f s b i -> (f s) b i")))
-        for pair in small:
-            nc.sync.dma_start(*pair)
+            return [(plane[row0 + r : P : 32], rows[r]) for r in range(4)]
 
         ident = keep.tile([P, P], F32, name="ident")
         make_identity(nc, ident[:])
 
-        w1c = keep.tile([P, COLD, S, 2 * H], U8, name="w1c", align_bytes=64)
-        w3c = keep.tile([P, COLD, S, 2 * H], U8, name="w3c", align_bytes=64)
+        w1c = {e: keep.tile([P, S, 2 * H], U8, name="w1_%d" % e, align_bytes=64) for e in range(1, E)}
+        w3c = {e: keep.tile([P, S, 2 * H], U8, name="w3_%d" % e, align_bytes=64) for e in range(1, E)}
         w2c = keep.tile([P, COLD, 2 * N], U8, name="w2c", align_bytes=64)
         w1h = keep.tile([P, S, 4 * H], U8, name="w1h", align_bytes=64)
-        w3h = keep.tile([P, S, 4 * H], U8, name="w3h", align_bytes=64)
+        w3h = keep.tile([P, S, 4 * H], U8, name="w3_0", align_bytes=64)
         w2h = keep.tile([P, 4 * N], U8, name="w2h", align_bytes=64)
         gate_sb = keep.tile([P, T], F32, name="gate_sb")
 
-        def cold(tile, dram, a, b):
-            return (tile[:, a:b].rearrange("p f s w -> p (f s) w").bitcast(I32),
-                    dram[a:b].bitcast(I32).rearrange("f s p w -> p (f s) w"))
+        def cold(tiles, dram, e):
+            return (tiles[e][:].bitcast(I32), dram[e - 1].bitcast(I32).rearrange("s p w -> p s w"))
 
-        def hot(tile, dram, s):
-            return (tile[:, s, :].bitcast(I32), dram[0, s].rearrange("p i d -> p (i d)").bitcast(I32))
+        def hot(tile, dram, a, b):
+            return (tile[:, a:b, :].bitcast(I32), dram[0, a:b].rearrange("s p i d -> p s (i d)").bitcast(I32))
 
-        def second(f):
-            cols = slice((f + 1) * C, (f + 2) * C)
-            return [(w2c[:, f, :].bitcast(I32), w2c_words[f, 0].bitcast(I32)), (gate_sb[:, cols], gate[:, cols])]
-
-        big = []
-        for f in range(COLD):
-            big += [cold(w1c, w1c_words, f, f + 1), cold(w3c, w3c_words, f, f + 1)]
-            if f == 0:
-                big += second(0)
-            if f >= 3:
-                big += second(f - 2)
-        rows1, rows3, rows2 = (scale_rows(sh1[:], 4, w1h_scales[0]), scale_rows(sh3[:], 8, w3h_scales[0]),
-                               scale_rows(sh2[:], 12, w2h_scales[0]))
-        big += rows1 + [hot(w1h, w1h_words, 0)] + rows3[:2] + [hot(w1h, w1h_words, 1)] + rows3[2:]
-        big += [hot(w1h, w1h_words, 2), hot(w3h, w3h_words, 0)] + rows2[:2] + [hot(w3h, w3h_words, 1)] + rows2[2:]
-        big += [hot(w3h, w3h_words, 2)] + second(COLD - 2) + second(COLD - 1) + [(w2h[:].bitcast(I32), w2h_words[0, 0].rearrange("p i d -> p (i d)").bitcast(I32)),
-                (gate_sb[:, 0:C], gate[:, 0:C])]
-        for pair in big:
+        order = [3, 4, 5, 1, 2, 0]
+        r_xs = scale_rows(xs_in[:].bitcast(I32), 0, x_scales)
+        r_c1 = scale_rows(sc1[:], 0, w1c_scales.rearrange("f s b i -> (f s) b i"))
+        r_c3 = scale_rows(sc3[:], 0, w3c_scales.rearrange("f s b i -> (f s) b i"))
+        r_c2 = scale_rows(sc2[:], 0, w2c_scales.rearrange("f s b i -> (f s) b i"))
+        r_h1, r_h3, r_h2 = (scale_rows(sh1, 4, w1h_scales[0]), scale_rows(sh3, 8, w3h_scales[0]),
+                            scale_rows(sh2, 12, w2h_scales[0]))
+        big1, big3 = [cold(w1c, w1c_words, e) for e in order[:5]], [cold(w3c, w3c_words, e) for e in order[:5]]
+        loads = [(xw_in[s][:, half], x_words[s].rearrange("p t d -> p (t d)").bitcast(I32)[:, half])
+                 for s in range(S) for half in (slice(0, T // 2), slice(T // 2, T))]
+        w2c_rows = w2c_words.bitcast(I32).rearrange("f s p w -> p (f s) w")
+        loads += [big1[0]] + r_xs + [(gate_rows[0:ROWS, 0:RUN], gate[0].rearrange("(r c) -> r c", r=ROWS))] + r_c1 + r_c3 + [big3[0]]
+        second = [(w2c[:, e - 1, :].bitcast(I32), w2c_rows[:, e - 1, :]) for e in order[:5]]
+        loads += r_c2[:2] + [big1[1], big3[1]] + r_c2[2:]
+        for step in (2, 3, 4):
+            loads += [big1[step], big3[step], second[step - 2]]
+        rows = r_h1 + r_h3 + r_h2
+        stream = [hot(w1h, w1h_words, s, s + 1) for s in range(S)] + [hot(w3h, w3h_words, s, s + 1) for s in range(S)]
+        for k, pair in enumerate(stream):
+            loads += rows[2 * k : 2 * k + 2] + [pair]
+        loads += second[3:] + [(w2h[:].bitcast(I32), w2h_words[0, 0].rearrange("p i d -> p (i d)").bitcast(I32))]
+        for pair in loads:
             nc.sync.dma_start(*pair)
 
-        groups = [(128, 384), (384, 768), (0, 128)]
-        gathered = {}
+        def spread_gate():
+            turned_gate = psum.tile([P, P], F32, name="t0")
+            nc.tensor.transpose(turned_gate[:], gate_rows[:], ident[:])
+            gate_cols = keep.tile([P, ROWS], F32, name="gate_cols")
+            nc.scalar.copy(gate_cols[:], turned_gate[:, 0:ROWS])
+            for k in range(2):
+                spread = psum.tile([P, 4, P], F32, name="y%d" % k)
+                for r in range(4):
+                    nc.tensor.transpose(spread[:, r, :], gate_cols[:, 4 * k + r : 4 * k + r + 1].to_broadcast([P, P]), ident[:])
+                nc.scalar.copy(gate_sb[:, 4 * k * RUN : 4 * (k + 1) * RUN].rearrange("p (r c) -> p r c", r=4), spread[:, :, 0:RUN])
 
-        def gather(a, b):
-            words = keep.tile([P, S, b - a], U32, name="xw_%d" % max(a, C), align_bytes=64)
-            scales = keep.tile([P, S, b - a], U8, name="xs_%d" % max(a, C), align_bytes=64)
-            sl = offsets[:, a // 16 : b // 16]
+        GROUP = 3 * C
+        words, scales = {}, {}
+
+        def gather_words(g, passes, place):
+            tile = keep.tile([P, len(passes), GROUP], U32, name=place, align_bytes=64)
+            for k, s in enumerate(passes):
+                words[g, s] = tile[:, k, :]
+                nc.vector.tensor_copy(words[g, s], xw_in[s][:].bitcast(U32).indirect(offsets[:, g * GROUP // 16 : (g + 1) * GROUP // 16]))
+
+        def gather_scales(g, place):
+            tile = keep.tile([P, S, GROUP], U8, name=place, align_bytes=64)
             for s in range(S):
-                nc.vector.tensor_copy(words[:, s, :], xw_in[s][:].bitcast(U32).indirect(sl))
-            for s in range(S):
-                nc.vector.tensor_copy(scales[:, s, :], xs_in[:, s, :].indirect(sl))
-            for e in range(a // C, b // C):
-                gathered[e] = (words, scales, slice(e * C - a, (e + 1) * C - a))
+                scales[g, s] = tile[:, s, :]
+                nc.vector.tensor_copy(scales[g, s], xs_in[:, s, :].indirect(offsets[:, g * GROUP // 16 : (g + 1) * GROUP // 16]))
 
         windows = [keep.tile([P, T], F32, name="window%d" % h) for h in range(2)]
 
-        def first_layer(e, step):
-            words, scales, cols = gathered[e]
-            banks = []
-            for wh, wc, sh, sc, row0, tag in ((w1h, w1c, sh1, sc1, 4, "a"), (w3h, w3c, sh3, sc3, 8, "b")):
-                acc = psum.tile([P, H], F32, name="%s%d" % (tag, step % 2))
-                for s in range(S):
-                    if e == 0:
-                        rhs, rs = wh[:, s, :].bitcast(FP8X4), sh[row0:P, s, :]
-                    else:
-                        rhs, rs = wc[:, e - 1, s, :].bitcast(FP4X4), sc[:, (e - 1) * S + s, :]
-                    nc.tensor.matmul_mx(acc[:], lhsT=words[:, s, cols].bitcast(FP8X4), lhsT_scale=scales[:, s, cols],
-                                        rhs=rhs, rhs_scale=rs, start=(s == 0), stop=(s == S - 1))
-                banks.append(acc)
+        def first_layer(e, wh, wc, row0, sc, tag):
+            g, cols = e // 3, slice((e % 3) * C, (e % 3 + 1) * C)
+            acc = psum.tile([P, H], F32, name=tag)
+            for s in range(S):
+                if e == 0:
+                    rhs, rs = wh[:, s, :].bitcast(FP8X4), hot_planes[row0:P, s, :].bitcast(U8)
+                else:
+                    rhs, rs = wc[e][:, s, :].bitcast(FP4X4), sc[:, (e - 1) * S + s, :].bitcast(U8)
+                nc.tensor.matmul_mx(acc[:], lhsT=words[g, s][:, cols].bitcast(FP8X4), lhsT_scale=scales[g, s][:, cols],
+                                    rhs=rhs, rhs_scale=rs, start=(s == 0), stop=(s == S - 1))
+            return acc
+
+        def gate_half(e, bank):
+            acc = first_layer(e, w1h, w1c, 4, sc1, bank)
             sg = work.tile([P, H], F32, name="sg")
-            nc.scalar.activation(sg[:], banks[0][:], SIGMOID)
+            nc.scalar.activation(sg[:], acc[:], SIGMOID)
+            return sg
+
+        def product(acc, sg):
             hid = work.tile([P, H], BF16, name="hid", align_bytes=64)
-            nc.vector.tensor_tensor(hid[:], banks[1][:], sg[:], MULT)
+            nc.vector.tensor_tensor(hid[:], acc[:], sg[:], MULT)
             return hid
 
-        def turn(hid, bank):
+        def turn(hid, turned):
             pairs = hid[:].bitcast(F32)
-            turned = psum.tile([P, 2, C], F32, name=bank)
             for u in range(2):
                 nc.tensor.transpose(turned[:, u, :], pairs[:, u : 2 * P : 2], ident[:])
+
+        def quantise(turned):
             grouped = work.tile([P, C * 4], BF16, name="grouped", align_bytes=64)
-            nc.scalar.copy(grouped[:].bitcast(F32).rearrange("p (c u) -> p c u", u=2), turned[:].rearrange("p u c -> p c u"))
-            hq = work.tile([P, C], U32, name="hq", align_bytes=64)
-            hs = work.tile([P, C], U8, name="hs", align_bytes=64)
+            nc.scalar.copy(grouped[:].bitcast(F32).rearrange("p (c u) -> p c u", u=2), turned.rearrange("p u c -> p c u"))
+            hq = work.tile([P, C], U32, name="hq", align_bytes=64, bufs=4)
+            hs = work.tile([P, C], U8, name="hs", align_bytes=64, bufs=4)
             nc.vector.quantize_mx(hq[:].bitcast(FP8X4), hs[:], grouped[:])
             return hq, hs
 
-        def second_layer(e, hq, hs):
-            y = psum.tile([P, 2, C], F32, name="y", bufs=2)
+        def second_layer(e, y, hq, hs):
             for h in range(2):
-                cols = slice(h * P, (h + 1) * P)
+                cols = slice(h * P // 4, (h + 1) * P // 4)
                 if e == 0:
                     lhsT, ls = w2h[:, h * 4 * P : (h + 1) * 4 * P].bitcast(FP8X4), sh2[12:P, 0, cols]
                 else:
                     lhsT, ls = w2c[:, e - 1, h * 2 * P : (h + 1) * 2 * P].bitcast(FP4X4), sc2[:, e - 1, cols]
-                nc.tensor.matmul_mx(y[:, h, :], lhsT=lhsT, lhsT_scale=ls, rhs=hq[:].bitcast(FP8X4), rhs_scale=hs[:],
+                nc.tensor.matmul_mx(y[:, h, :], lhsT=lhsT, lhsT_scale=ls.bitcast(U8), rhs=hq[:].bitcast(FP8X4), rhs_scale=hs[:],
                                     start=True, stop=True)
-            ysb = work.tile([P, 2, C], F32, name="ysb")
-            nc.scalar.copy(ysb[:], y[:])
-            return ysb
 
-        def scatter(e, ysb):
+        def scatter(e, y):
+            ysb = work.tile([P, 2, C], F32, name="ysb")
+            nc.scalar.copy(ysb[:], y)
             sl = offsets[:, e * C // 16 : (e + 1) * C // 16]
             for h in range(2):
                 nc.vector.tensor_tensor(windows[h][:].indirect(sl), ysb[:, h, :], gate_sb[:, e * C : (e + 1) * C], MULT)
 
-        for group in groups[:2]:
-            gather(*group)
-        order = [1, 2, 3, 4, 5, 0]
-        hids, codes = {}, {}
-        for step in range(len(order) + 2):
-            if step < len(order):
-                hids[step] = first_layer(order[step], step)
-            if 1 <= step <= len(order):
-                codes[step - 1] = turn(hids[step - 1], "a%d" % (step % 2))
-            if step >= 2:
-                scatter(order[step - 2], second_layer(order[step - 2], *codes[step - 2]))
-            if step == 1:
-                gather(*groups[2])
+        def finish(step, bank):
+            y = psum.tile([P, 2, C], F32, name=bank)
+            second_layer(order[step], y[:], *codes[step])
+            scatter(order[step], y[:])
+
+        spread_gate()
+        gather_words(1, (0, 1, 2), "xw_1")
+        gather_scales(1, "xs_1")
+        gather_words(0, (0,), "xw_0")
+        last = len(order) - 1
+        codes, hids = {}, {}
+        for step in range(last + 1):
+            sg = gate_half(order[step], "a%d" % (step % 2))
+            if step == 0:
+                gather_words(0, (1, 2), "w1_%d" % order[0])
+            hids[step] = hid = product(first_layer(order[step], w3h, w3c, 8, sc3, "b%d" % (step % 2)), sg)
+            if step == 0:
+                gather_scales(0, "w3_%d" % order[0])
+            if step >= 1:
+                turned = psum.tile([P, 2, C], F32, name="a%d" % (step % 2))
+                turn(hids[step - 1], turned[:])
+                codes[step - 1] = quantise(turned[:])
+                if step >= 2:
+                    finish(step - 2, "y%d" % (step % 2))
+        turned = psum.tile([P, 2, C], F32, name="t0")
+        turn(hids[last], turned[:])
+        codes[last] = quantise(turned[:])
+        finish(last - 1, "y0")
+        finish(last, "y1")
         for h in range(2):
             nc.sync.dma_start(out[h * P : (h + 1) * P, :], windows[h][:])

@@ -37,26 +37,27 @@ def tile_moe_hot_glu_sigmoid_kernel(
         nc.sync.dma_start(offsets[:], offs)
 
         xw_in = [keep.tile([P, T], I32, name="xw_in%d" % s, align_bytes=64) for s in range(S)]
-        xs_in = keep.tile([P, S, T], U8, name="xs_in", align_bytes=64)
+        xs_in = keep.tile([P, S, T // 4], I32, name="xs_in", align_bytes=64)
         sc1 = keep.tile([P, COLD * S, H // 4], I32, name="sc1", align_bytes=64)
         sc3 = keep.tile([P, COLD * S, H // 4], I32, name="sc3", align_bytes=64)
         sc2 = keep.tile([P, COLD, N // 4], I32, name="sc2", align_bytes=64)
-        hot_planes = keep.tile([P, S, H // 4], I32, name="hot_planes", align_bytes=64)
+        hot_planes = keep.tile([P, S, H], U8, name="hot_planes", align_bytes=64)
         gate_rows = keep.tile([P, P], F32, name="gate_rows")
-        nc.gpsimd.memset(xs_in[:].rearrange("p g w -> p (g w)").bitcast(I32), 0)
+        ident = keep.tile([P, P], F32, name="ident")
         nc.gpsimd.memset(gate_rows[:], 0.0)
-        for plane in (sc1, sc3, sc2, hot_planes):
-            nc.vector.memset(plane[:].rearrange("p g w -> p (g w)"), 0)
-        sh1, sh3, sh2 = hot_planes[:], hot_planes[:], hot_planes[:, 0:1, 0 : N // 4]
+        make_identity(nc, ident[:])
+        for plane in (xs_in[:], sc1[:], sc3[:], sc2[:], hot_planes[:].bitcast(I32)):
+            nc.vector.memset(plane.rearrange("p g w -> p (g w)"), 0)
+        sh1 = sh3 = hot_planes[:].bitcast(I32)
+        sh2 = hot_planes[:, 0:1, 0:N].bitcast(I32)
 
         def scale_rows(plane, row0, dram):
             rows = dram.bitcast(I32).rearrange("g (q r) w -> r q g w", r=4)
             return [(plane[row0 + r : P : 32], rows[r]) for r in range(4)]
 
-        ident = keep.tile([P, P], F32, name="ident")
-        make_identity(nc, ident[:])
-
-        w1c = {e: keep.tile([P, S, 2 * H], U8, name="w1_%d" % e, align_bytes=64) for e in range(1, E)}
+        order = [3, 4, 5, 1, 2, 0]
+        w1c = {e: keep.tile([P, S, 2 * H], U8, name="w1_%d" % e, align_bytes=64) for e in order[1:5]}
+        first = [keep.tile([P, 2 * H], U8, name="first%d" % s, align_bytes=64) for s in range(S)]
         w3c = {e: keep.tile([P, S, 2 * H], U8, name="w3_%d" % e, align_bytes=64) for e in range(1, E)}
         w2c = keep.tile([P, COLD, 2 * N], U8, name="w2c", align_bytes=64)
         w1h = keep.tile([P, S, 4 * H], U8, name="w1h", align_bytes=64)
@@ -70,20 +71,18 @@ def tile_moe_hot_glu_sigmoid_kernel(
         def hot(tile, dram, a, b):
             return (tile[:, a:b, :].bitcast(I32), dram[0, a:b].rearrange("s p i d -> p s (i d)").bitcast(I32))
 
-        order = [3, 4, 5, 1, 2, 0]
-        r_xs = scale_rows(xs_in[:].bitcast(I32), 0, x_scales)
+        r_xs = scale_rows(xs_in[:], 0, x_scales)
         r_c1 = scale_rows(sc1[:], 0, w1c_scales.rearrange("f s b i -> (f s) b i"))
         r_c3 = scale_rows(sc3[:], 0, w3c_scales.rearrange("f s b i -> (f s) b i"))
         r_c2 = scale_rows(sc2[:], 0, w2c_scales.rearrange("f s b i -> (f s) b i"))
         r_h1, r_h3, r_h2 = (scale_rows(sh1, 4, w1h_scales[0]), scale_rows(sh3, 8, w3h_scales[0]),
                             scale_rows(sh2, 12, w2h_scales[0]))
-        big1, big3 = [cold(w1c, w1c_words, e) for e in order[:5]], [cold(w3c, w3c_words, e) for e in order[:5]]
-        loads = [(xw_in[s][:, half], x_words[s].rearrange("p t d -> p (t d)").bitcast(I32)[:, half])
-                 for s in range(S) for half in (slice(0, T // 2), slice(T // 2, T))]
+        big1, big3 = [None] + [cold(w1c, w1c_words, e) for e in order[1:5]], [cold(w3c, w3c_words, e) for e in order[:5]]
+        loads = [(xw_in[s][:], x_words[s].rearrange("p t d -> p (t d)").bitcast(I32)) for s in range(S)]
         w2c_rows = w2c_words.bitcast(I32).rearrange("f s p w -> p (f s) w")
-        loads += [big1[0]] + r_xs + [(gate_rows[0:ROWS, 0:RUN], gate[0].rearrange("(r c) -> r c", r=ROWS))] + r_c1 + r_c3 + [big3[0]]
+        loads += r_xs + [(first[s][:].bitcast(I32), w1c_words[order[0] - 1, s].bitcast(I32)) for s in range(S)] + [(gate_rows[0:ROWS, 0:RUN], gate[0].rearrange("(r c) -> r c", r=ROWS))] + r_c1 + [big3[0]] + r_c3
         second = [(w2c[:, e - 1, :].bitcast(I32), w2c_rows[:, e - 1, :]) for e in order[:5]]
-        loads += r_c2[:2] + [big1[1], big3[1]] + r_c2[2:]
+        loads += [big1[1], big3[1]] + r_c2
         for step in (2, 3, 4):
             loads += [big1[step], big3[step], second[step - 2]]
         rows = r_h1 + r_h3 + r_h2
@@ -114,11 +113,11 @@ def tile_moe_hot_glu_sigmoid_kernel(
                 words[g, s] = tile[:, k, :]
                 nc.vector.tensor_copy(words[g, s], xw_in[s][:].bitcast(U32).indirect(offsets[:, g * GROUP // 16 : (g + 1) * GROUP // 16]))
 
-        def gather_scales(g, place):
-            tile = keep.tile([P, S, GROUP], U8, name=place, align_bytes=64)
-            for s in range(S):
-                scales[g, s] = tile[:, s, :]
-                nc.vector.tensor_copy(scales[g, s], xs_in[:, s, :].indirect(offsets[:, g * GROUP // 16 : (g + 1) * GROUP // 16]))
+        def gather_scales(g, passes, place):
+            tile = keep.tile([P, len(passes), GROUP], U8, name=place, align_bytes=64)
+            for k, s in enumerate(passes):
+                scales[g, s] = tile[:, k, :]
+                nc.vector.tensor_copy(scales[g, s], xs_in[:, s, :].bitcast(U8).indirect(offsets[:, g * GROUP // 16 : (g + 1) * GROUP // 16]))
 
         windows = [keep.tile([P, T], F32, name="window%d" % h) for h in range(2)]
 
@@ -127,9 +126,9 @@ def tile_moe_hot_glu_sigmoid_kernel(
             acc = psum.tile([P, H], F32, name=tag)
             for s in range(S):
                 if e == 0:
-                    rhs, rs = wh[:, s, :].bitcast(FP8X4), hot_planes[row0:P, s, :].bitcast(U8)
+                    rhs, rs = wh[:, s, :].bitcast(FP8X4), hot_planes[row0:P, s, :]
                 else:
-                    rhs, rs = wc[e][:, s, :].bitcast(FP4X4), sc[:, (e - 1) * S + s, :].bitcast(U8)
+                    rhs, rs = (wc[e][:, s, :] if e in wc else first[s][:]).bitcast(FP4X4), sc[:, (e - 1) * S + s, :].bitcast(U8)
                 nc.tensor.matmul_mx(acc[:], lhsT=words[g, s][:, cols].bitcast(FP8X4), lhsT_scale=scales[g, s][:, cols],
                                     rhs=rhs, rhs_scale=rs, start=(s == 0), stop=(s == S - 1))
             return acc
@@ -182,17 +181,17 @@ def tile_moe_hot_glu_sigmoid_kernel(
 
         spread_gate()
         gather_words(1, (0, 1, 2), "xw_1")
-        gather_scales(1, "xs_1")
-        gather_words(0, (0,), "xw_0")
+        gather_scales(1, (0, 1, 2), "xs_1")
         last = len(order) - 1
         codes, hids = {}, {}
         for step in range(last + 1):
             sg = gate_half(order[step], "a%d" % (step % 2))
             if step == 0:
-                gather_words(0, (1, 2), "w1_%d" % order[0])
+                for s in range(S):
+                    gather_words(0, (s,), "first%d" % s)
             hids[step] = hid = product(first_layer(order[step], w3h, w3c, 8, sc3, "b%d" % (step % 2)), sg)
-            if step == 0:
-                gather_scales(0, "w3_%d" % order[0])
+            if step < 2:
+                gather_scales(0, ((0, 1), (2,))[step], "w3_%d" % order[step])
             if step >= 1:
                 turned = psum.tile([P, 2, C], F32, name="a%d" % (step % 2))
                 turn(hids[step - 1], turned[:])

@@ -41,15 +41,15 @@ def tile_moe_hot_glu_sigmoid_kernel(
         sc1 = keep.tile([P, COLD * S, H // 4], I32, name="sc1", align_bytes=64)
         sc3 = keep.tile([P, COLD * S, H // 4], I32, name="sc3", align_bytes=64)
         sc2 = keep.tile([P, COLD, N // 4], I32, name="sc2", align_bytes=64)
-        hot_planes = keep.tile([P, S, H], U8, name="hot_planes", align_bytes=64)
+        hot_planes = keep.tile([P, S, H // 4], I32, name="hot_planes", align_bytes=64)
         gate_rows = keep.tile([P, P], F32, name="gate_rows")
         ident = keep.tile([P, P], F32, name="ident")
         nc.gpsimd.memset(gate_rows[:], 0.0)
         make_identity(nc, ident[:])
-        for plane in (xs_in[:], sc1[:], sc3[:], sc2[:], hot_planes[:].bitcast(I32)):
+        for plane in (xs_in[:], sc1[:], hot_planes[:], sc3[:], sc2[:]):
             nc.vector.memset(plane.rearrange("p g w -> p (g w)"), 0)
-        sh1 = sh3 = hot_planes[:].bitcast(I32)
-        sh2 = hot_planes[:, 0:1, 0:N].bitcast(I32)
+        sh1 = sh3 = hot_planes[:]
+        sh2 = hot_planes[:, 0:1, 0 : N // 4]
 
         def scale_rows(plane, row0, dram):
             rows = dram.bitcast(I32).rearrange("g (q r) w -> r q g w", r=4)
@@ -79,16 +79,18 @@ def tile_moe_hot_glu_sigmoid_kernel(
                             scale_rows(sh2, 12, w2h_scales[0]))
         big1, big3 = [None] + [cold(w1c, w1c_words, e) for e in order[1:5]], [cold(w3c, w3c_words, e) for e in order[:5]]
         loads = [(xw_in[s][:], x_words[s].rearrange("p t d -> p (t d)").bitcast(I32)) for s in range(S)]
+        loads = loads[:1] + [(gate_rows[0:ROWS, 0:RUN], gate[0].rearrange("(r c) -> r c", r=ROWS))] + loads[1:]
         w2c_rows = w2c_words.bitcast(I32).rearrange("f s p w -> p (f s) w")
-        loads += r_xs + [(first[s][:].bitcast(I32), w1c_words[order[0] - 1, s].bitcast(I32)) for s in range(S)] + [(gate_rows[0:ROWS, 0:RUN], gate[0].rearrange("(r c) -> r c", r=ROWS))] + r_c1 + [big3[0]] + r_c3
+        loads += [(first[s][:].bitcast(I32), w1c_words[order[0] - 1, s].bitcast(I32)) for s in range(S)] + [big3[0]]
+        loads += r_xs
+        for rows in ((r_c1, r_h1, r_h2), (r_c3, r_h3, r_c2)):
+            for r in range(4):
+                loads += [plane[r] for plane in rows]
         second = [(w2c[:, e - 1, :].bitcast(I32), w2c_rows[:, e - 1, :]) for e in order[:5]]
-        loads += [big1[1], big3[1]] + r_c2
+        loads += [big1[1], big3[1]]
         for step in (2, 3, 4):
             loads += [big1[step], big3[step], second[step - 2]]
-        rows = r_h1 + r_h3 + r_h2
-        stream = [hot(w1h, w1h_words, s, s + 1) for s in range(S)] + [hot(w3h, w3h_words, s, s + 1) for s in range(S)]
-        for k, pair in enumerate(stream):
-            loads += rows[2 * k : 2 * k + 2] + [pair]
+        loads += [hot(w1h, w1h_words, 0, S), hot(w3h, w3h_words, 0, S - 1), hot(w3h, w3h_words, S - 1, S)]
         loads += second[3:] + [(w2h[:].bitcast(I32), w2h_words[0, 0].rearrange("p i d -> p (i d)").bitcast(I32))]
         for pair in loads:
             nc.sync.dma_start(*pair)
@@ -126,7 +128,7 @@ def tile_moe_hot_glu_sigmoid_kernel(
             acc = psum.tile([P, H], F32, name=tag)
             for s in range(S):
                 if e == 0:
-                    rhs, rs = wh[:, s, :].bitcast(FP8X4), hot_planes[row0:P, s, :]
+                    rhs, rs = wh[:, s, :].bitcast(FP8X4), hot_planes[row0:P, s, :].bitcast(U8)
                 else:
                     rhs, rs = (wc[e][:, s, :] if e in wc else first[s][:]).bitcast(FP4X4), sc[:, (e - 1) * S + s, :].bitcast(U8)
                 nc.tensor.matmul_mx(acc[:], lhsT=words[g, s][:, cols].bitcast(FP8X4), lhsT_scale=scales[g, s][:, cols],
@@ -181,14 +183,15 @@ def tile_moe_hot_glu_sigmoid_kernel(
 
         spread_gate()
         gather_words(1, (0, 1, 2), "xw_1")
+        gather_words(0, (0,), "xw_0")
         gather_scales(1, (0, 1, 2), "xs_1")
         last = len(order) - 1
         codes, hids = {}, {}
         for step in range(last + 1):
             sg = gate_half(order[step], "a%d" % (step % 2))
             if step == 0:
-                for s in range(S):
-                    gather_words(0, (s,), "first%d" % s)
+                for s in range(1, S):
+                    gather_words(0, (s,), "first%d" % (s - 1))
             hids[step] = hid = product(first_layer(order[step], w3h, w3c, 8, sc3, "b%d" % (step % 2)), sg)
             if step < 2:
                 gather_scales(0, ((0, 1), (2,))[step], "w3_%d" % order[step])

@@ -183,18 +183,14 @@ def tile_moe_hot_glu_sigmoid_kernel(
 
         spread_gate()
         gather_words(1, (0, 1, 2), "xw_1")
-        gather_words(0, (0,), "xw_0")
+        gather_words(0, (0, 1, 2), "xw_0")
         gather_scales(1, (0, 1, 2), "xs_1")
+        gather_scales(0, (0, 1, 2), "xs_0")
         last = len(order) - 1
         codes, hids = {}, {}
         for step in range(last + 1):
             sg = gate_half(order[step], "a%d" % (step % 2))
-            if step == 0:
-                for s in range(1, S):
-                    gather_words(0, (s,), "first%d" % (s - 1))
             hids[step] = hid = product(first_layer(order[step], w3h, w3c, 8, sc3, "b%d" % (step % 2)), sg)
-            if step < 2:
-                gather_scales(0, ((0, 1), (2,))[step], "w3_%d" % order[step])
             if step >= 1:
                 turned = psum.tile([P, 2, C], F32, name="a%d" % (step % 2))
                 turn(hids[step - 1], turned[:])

@@ -16,11 +16,14 @@ FP8X4 = mybir.dt.float8_e4m3fn_x4
 FP4X4 = mybir.dt.float4_e2m1fn_x4
 MULT = mybir.AluOpType.mult
 SIGMOID = mybir.ActivationFunctionType.Sigmoid
+COPY = mybir.ActivationFunctionType.Copy
 
 P = 128
 S = K // 512
 COLD = E - 1
 ROWS, RUN = 8, T // 8
+GROUP = 3 * C
+ORDER = [3, 4, 5, 1, 2, 0]
 
 
 def tile_moe_hot_glu_sigmoid_kernel(
@@ -48,20 +51,18 @@ def tile_moe_hot_glu_sigmoid_kernel(
         make_identity(nc, ident[:])
         for plane in (xs_in[:], sc1[:], hot_planes[:], sc3[:], sc2[:]):
             nc.vector.memset(plane.rearrange("p g w -> p (g w)"), 0)
-        sh1 = sh3 = hot_planes[:]
         sh2 = hot_planes[:, 0:1, 0 : N // 4]
 
         def scale_rows(plane, row0, dram):
             rows = dram.bitcast(I32).rearrange("g (q r) w -> r q g w", r=4)
             return [(plane[row0 + r : P : 32], rows[r]) for r in range(4)]
 
-        order = [3, 4, 5, 1, 2, 0]
-        w1c = {e: keep.tile([P, S, 2 * H], U8, name="w1_%d" % e, align_bytes=64) for e in order[1:5]}
         first = [keep.tile([P, 2 * H], U8, name="first%d" % s, align_bytes=64) for s in range(S)]
-        w3c = {e: keep.tile([P, S, 2 * H], U8, name="w3_%d" % e, align_bytes=64) for e in range(1, E)}
-        w2c = keep.tile([P, COLD, 2 * N], U8, name="w2c", align_bytes=64)
+        w1c = {e: keep.tile([P, S, 2 * H], U8, name="w1_%d" % e, align_bytes=64) for e in ORDER[1:5]}
+        w3c = {e: keep.tile([P, S, 2 * H], U8, name="w3_%d" % e, align_bytes=64) for e in ORDER[:5]}
+        w2c = {e: keep.tile([P, 2 * N], U8, name="w2_%d" % e, align_bytes=64) for e in ORDER[:5]}
         w1h = keep.tile([P, S, 4 * H], U8, name="w1h", align_bytes=64)
-        w3h = keep.tile([P, S, 4 * H], U8, name="w3_0", align_bytes=64)
+        w3h = keep.tile([P, S, 4 * H], U8, name="w3h", align_bytes=64)
         w2h = keep.tile([P, 4 * N], U8, name="w2h", align_bytes=64)
         gate_sb = keep.tile([P, T], F32, name="gate_sb")
 
@@ -75,57 +76,53 @@ def tile_moe_hot_glu_sigmoid_kernel(
         r_c1 = scale_rows(sc1[:], 0, w1c_scales.rearrange("f s b i -> (f s) b i"))
         r_c3 = scale_rows(sc3[:], 0, w3c_scales.rearrange("f s b i -> (f s) b i"))
         r_c2 = scale_rows(sc2[:], 0, w2c_scales.rearrange("f s b i -> (f s) b i"))
-        r_h1, r_h3, r_h2 = (scale_rows(sh1, 4, w1h_scales[0]), scale_rows(sh3, 8, w3h_scales[0]),
-                            scale_rows(sh2, 12, w2h_scales[0]))
-        big1, big3 = [None] + [cold(w1c, w1c_words, e) for e in order[1:5]], [cold(w3c, w3c_words, e) for e in order[:5]]
+        r_h1 = scale_rows(hot_planes[:], 4, w1h_scales[0])
+        r_h3 = scale_rows(hot_planes[:], 8, w3h_scales[0])
+        r_h2 = scale_rows(sh2, 12, w2h_scales[0])
         loads = [(xw_in[s][:], x_words[s].rearrange("p t d -> p (t d)").bitcast(I32)) for s in range(S)]
         loads = loads[:1] + [(gate_rows[0:ROWS, 0:RUN], gate[0].rearrange("(r c) -> r c", r=ROWS))] + loads[1:]
-        w2c_rows = w2c_words.bitcast(I32).rearrange("f s p w -> p (f s) w")
-        loads += [(first[s][:].bitcast(I32), w1c_words[order[0] - 1, s].bitcast(I32)) for s in range(S)] + [big3[0]]
+        loads += [(first[s][:].bitcast(I32), w1c_words[ORDER[0] - 1, s].bitcast(I32)) for s in range(S)]
+        loads += [cold(w3c, w3c_words, ORDER[0])]
         loads += r_xs
         for rows in ((r_c1, r_h1, r_h2), (r_c3, r_h3, r_c2)):
             for r in range(4):
                 loads += [plane[r] for plane in rows]
-        second = [(w2c[:, e - 1, :].bitcast(I32), w2c_rows[:, e - 1, :]) for e in order[:5]]
-        loads += [big1[1], big3[1]]
-        for step in (2, 3, 4):
-            loads += [big1[step], big3[step], second[step - 2]]
-        loads += [hot(w1h, w1h_words, 0, S), hot(w3h, w3h_words, 0, S - 1), hot(w3h, w3h_words, S - 1, S)]
-        loads += second[3:] + [(w2h[:].bitcast(I32), w2h_words[0, 0].rearrange("p i d -> p (i d)").bitcast(I32))]
+        second = [(w2c[e][:].bitcast(I32), w2c_words[e - 1, 0].bitcast(I32)) for e in ORDER[:5]]
+        for step in range(1, 5):
+            loads += [cold(w1c, w1c_words, ORDER[step])] + second[step - 2 : step - 1] + [cold(w3c, w3c_words, ORDER[step])]
+        loads += [hot(w1h, w1h_words, 0, S), second[3], hot(w3h, w3h_words, 0, S - 1), second[4], hot(w3h, w3h_words, S - 1, S)]
+        loads += [(w2h[:].bitcast(I32), w2h_words[0, 0].rearrange("p i d -> p (i d)").bitcast(I32))]
         for pair in loads:
             nc.sync.dma_start(*pair)
 
-        def spread_gate():
-            turned_gate = psum.tile([P, P], F32, name="t0")
-            nc.tensor.transpose(turned_gate[:], gate_rows[:], ident[:])
-            gate_cols = keep.tile([P, ROWS], F32, name="gate_cols")
-            nc.scalar.copy(gate_cols[:], turned_gate[:, 0:ROWS])
-            for k in range(2):
-                spread = psum.tile([P, 4, P], F32, name="y%d" % k)
-                for r in range(4):
-                    nc.tensor.transpose(spread[:, r, :], gate_cols[:, 4 * k + r : 4 * k + r + 1].to_broadcast([P, P]), ident[:])
-                nc.scalar.copy(gate_sb[:, 4 * k * RUN : 4 * (k + 1) * RUN].rearrange("p (r c) -> p r c", r=4), spread[:, :, 0:RUN])
+        turned_gate = psum.tile([P, P], F32, name="t0")
+        nc.tensor.transpose(turned_gate[:], gate_rows[:], ident[:])
+        gate_cols = keep.tile([P, ROWS], F32, name="gate_cols")
+        nc.scalar.copy(gate_cols[:], turned_gate[:, 0:ROWS])
+        for k in range(2):
+            spread = psum.tile([P, 4, P], F32, name="y%d" % k)
+            for r in range(4):
+                nc.tensor.transpose(spread[:, r, :], gate_cols[:, 4 * k + r : 4 * k + r + 1].to_broadcast([P, P]), ident[:])
+            nc.scalar.copy(gate_sb[:, 4 * k * RUN : 4 * (k + 1) * RUN].rearrange("p (r c) -> p r c", r=4), spread[:, :, 0:RUN])
 
-        GROUP = 3 * C
         words, scales = {}, {}
 
-        def gather_words(g, passes, place):
-            tile = keep.tile([P, len(passes), GROUP], U32, name=place, align_bytes=64)
-            for k, s in enumerate(passes):
-                words[g, s] = tile[:, k, :]
-                nc.vector.tensor_copy(words[g, s], xw_in[s][:].bitcast(U32).indirect(offsets[:, g * GROUP // 16 : (g + 1) * GROUP // 16]))
+        def gather(found, g, dtype, name, windows_in):
+            tile = keep.tile([P, S, GROUP], dtype, name=name, align_bytes=64)
+            for s in range(S):
+                found[g, s] = tile[:, s, :]
+                nc.vector.tensor_copy(found[g, s], windows_in[s].bitcast(dtype).indirect(offsets[:, g * GROUP // 16 : (g + 1) * GROUP // 16]))
 
-        def gather_scales(g, passes, place):
-            tile = keep.tile([P, len(passes), GROUP], U8, name=place, align_bytes=64)
-            for k, s in enumerate(passes):
-                scales[g, s] = tile[:, k, :]
-                nc.vector.tensor_copy(scales[g, s], xs_in[:, s, :].bitcast(U8).indirect(offsets[:, g * GROUP // 16 : (g + 1) * GROUP // 16]))
+        for g in (1, 0):
+            gather(words, g, U32, "xw_%d" % g, [xw_in[s][:] for s in range(S)])
+        for g in (1, 0):
+            gather(scales, g, U8, "xs_%d" % g, [xs_in[:, s, :] for s in range(S)])
 
         windows = [keep.tile([P, T], F32, name="window%d" % h) for h in range(2)]
 
-        def first_layer(e, wh, wc, row0, sc, tag):
+        def first_layer(e, wh, wc, row0, sc, bank):
             g, cols = e // 3, slice((e % 3) * C, (e % 3 + 1) * C)
-            acc = psum.tile([P, H], F32, name=tag)
+            acc = psum.tile([P, H], F32, name=bank)
             for s in range(S):
                 if e == 0:
                     rhs, rs = wh[:, s, :].bitcast(FP8X4), hot_planes[row0:P, s, :].bitcast(U8)
@@ -133,74 +130,68 @@ def tile_moe_hot_glu_sigmoid_kernel(
                     rhs, rs = (wc[e][:, s, :] if e in wc else first[s][:]).bitcast(FP4X4), sc[:, (e - 1) * S + s, :].bitcast(U8)
                 nc.tensor.matmul_mx(acc[:], lhsT=words[g, s][:, cols].bitcast(FP8X4), lhsT_scale=scales[g, s][:, cols],
                                     rhs=rhs, rhs_scale=rs, start=(s == 0), stop=(s == S - 1))
-            return acc
+            return acc[:].rearrange("c (p u v) -> c u p v", u=2, v=2)
 
-        def gate_half(e, bank):
-            acc = first_layer(e, w1h, w1c, 4, sc1, bank)
-            sg = work.tile([P, H], F32, name="sg")
-            nc.scalar.activation(sg[:], acc[:], SIGMOID)
+        def gate_half(step):
+            acc = first_layer(ORDER[step], w1h, w1c, 4, sc1, "a%d" % (step % 2))
+            sg = work.tile([P, 2, P, 2], F32, name="sg")
+            nc.scalar.activation(sg[:], acc, SIGMOID)
             return sg
 
-        def product(acc, sg):
-            hid = work.tile([P, H], BF16, name="hid", align_bytes=64)
-            nc.vector.tensor_tensor(hid[:], acc[:], sg[:], MULT)
+        def product(step, sg):
+            acc = first_layer(ORDER[step], w3h, w3c, 8, sc3, "b%d" % (step % 2))
+            hid = work.tile([P, 2, P, 2], BF16, name="hid", align_bytes=64)
+            nc.vector.tensor_tensor(hid[:], acc, sg[:], MULT)
             return hid
 
-        def turn(hid, turned):
-            pairs = hid[:].bitcast(F32)
+        def quantise(hid, turned):
+            pairs = hid[:].rearrange("c u p v -> c (u p v)").bitcast(F32)
             for u in range(2):
-                nc.tensor.transpose(turned[:, u, :], pairs[:, u : 2 * P : 2], ident[:])
-
-        def quantise(turned):
+                nc.tensor.transpose(turned[:, u, :], pairs[:, u * P : (u + 1) * P], ident[:])
             grouped = work.tile([P, C * 4], BF16, name="grouped", align_bytes=64)
-            nc.scalar.copy(grouped[:].bitcast(F32).rearrange("p (c u) -> p c u", u=2), turned.rearrange("p u c -> p c u"))
-            hq = work.tile([P, C], U32, name="hq", align_bytes=64, bufs=4)
-            hs = work.tile([P, C], U8, name="hs", align_bytes=64, bufs=4)
+            nc.vector.tensor_copy(grouped[:].bitcast(F32).rearrange("p (c u) -> p c u", u=2), turned.rearrange("p u c -> p c u"))
+            hq = work.tile([P, C], U32, name="hq", align_bytes=64)
+            hs = work.tile([P, C], U8, name="hs", align_bytes=64)
             nc.vector.quantize_mx(hq[:].bitcast(FP8X4), hs[:], grouped[:])
             return hq, hs
 
-        def second_layer(e, y, hq, hs):
+        def second_layer(step, ys, hq, hs):
+            e = ORDER[step]
             for h in range(2):
                 cols = slice(h * P // 4, (h + 1) * P // 4)
                 if e == 0:
                     lhsT, ls = w2h[:, h * 4 * P : (h + 1) * 4 * P].bitcast(FP8X4), sh2[12:P, 0, cols]
                 else:
-                    lhsT, ls = w2c[:, e - 1, h * 2 * P : (h + 1) * 2 * P].bitcast(FP4X4), sc2[:, e - 1, cols]
-                nc.tensor.matmul_mx(y[:, h, :], lhsT=lhsT, lhsT_scale=ls.bitcast(U8), rhs=hq[:].bitcast(FP8X4), rhs_scale=hs[:],
+                    lhsT, ls = w2c[e][:, h * 2 * P : (h + 1) * 2 * P].bitcast(FP4X4), sc2[:, e - 1, cols]
+                nc.tensor.matmul_mx(ys[h], lhsT=lhsT, lhsT_scale=ls.bitcast(U8), rhs=hq[:].bitcast(FP8X4), rhs_scale=hs[:],
                                     start=True, stop=True)
 
-        def scatter(e, y):
-            ysb = work.tile([P, 2, C], F32, name="ysb")
-            nc.scalar.copy(ysb[:], y)
-            sl = offsets[:, e * C // 16 : (e + 1) * C // 16]
-            for h in range(2):
-                nc.vector.tensor_tensor(windows[h][:].indirect(sl), ysb[:, h, :], gate_sb[:, e * C : (e + 1) * C], MULT)
+        def slots(step):
+            e = ORDER[step]
+            return gate_sb[:, e * C : (e + 1) * C], offsets[:, e * C // 16 : (e + 1) * C // 16]
 
-        def finish(step, bank):
-            y = psum.tile([P, 2, C], F32, name=bank)
-            second_layer(order[step], y[:], *codes[step])
-            scatter(order[step], y[:])
+        def scatter(step, y):
+            weight, listed = slots(step)
+            gated = work.tile([P, 2, C], F32, name="gated")
+            nc.vector.tensor_tensor(gated[:], y, weight.unsqueeze(1).to_broadcast([P, 2, C]), MULT)
+            nc.scalar.activation(windows[0][:].indirect(listed), gated[:, 0, :], COPY)
+            if step < E - 1:
+                nc.scalar.activation(windows[1][:].indirect(listed), gated[:, 1, :], COPY)
+            else:
+                nc.vector.tensor_copy(windows[1][:].indirect(listed), gated[:, 1, :])
 
-        spread_gate()
-        gather_words(1, (0, 1, 2), "xw_1")
-        gather_words(0, (0, 1, 2), "xw_0")
-        gather_scales(1, (0, 1, 2), "xs_1")
-        gather_scales(0, (0, 1, 2), "xs_0")
-        last = len(order) - 1
-        codes, hids = {}, {}
-        for step in range(last + 1):
-            sg = gate_half(order[step], "a%d" % (step % 2))
-            hids[step] = hid = product(first_layer(order[step], w3h, w3c, 8, sc3, "b%d" % (step % 2)), sg)
-            if step >= 1:
-                turned = psum.tile([P, 2, C], F32, name="a%d" % (step % 2))
-                turn(hids[step - 1], turned[:])
-                codes[step - 1] = quantise(turned[:])
-                if step >= 2:
-                    finish(step - 2, "y%d" % (step % 2))
-        turned = psum.tile([P, 2, C], F32, name="t0")
-        turn(hids[last], turned[:])
-        codes[last] = quantise(turned[:])
-        finish(last - 1, "y0")
-        finish(last, "y1")
+        hids, codes = {}, {}
+        for step in range(E + 2):
+            if step < E:
+                sg = gate_half(step)
+            if step >= 2:
+                y = psum.tile([P, 2, C], F32, name="y%d" % (step % 2))
+                second_layer(step - 2, (y[:, 0, :], y[:, 1, :]), *codes[step - 2])
+                scatter(step - 2, y[:])
+            if 1 <= step <= E:
+                turned = psum.tile([P, 2, C], F32, name="a1" if step == 1 else "t%d" % (step % 2))
+                codes[step - 1] = quantise(hids[step - 1], turned[:])
+            if step < E:
+                hids[step] = product(step, sg)
         for h in range(2):
             nc.sync.dma_start(out[h * P : (h + 1) * P, :], windows[h][:])

@@ -49,8 +49,13 @@ def tile_moe_hot_glu_sigmoid_kernel(
         ident = keep.tile([P, P], F32, name="ident")
         nc.gpsimd.memset(gate_rows[:], 0.0)
         make_identity(nc, ident[:])
-        for plane in (xs_in[:], sc1[:], hot_planes[:], sc3[:], sc2[:]):
+        zero = keep.tile([P, 8], I32, name="zero")
+        nc.vector.memset(zero[:], 0)
+        for plane in (xs_in[:], hot_planes[:], sc2[:]):
             nc.vector.memset(plane.rearrange("p g w -> p (g w)"), 0)
+        for plane in (sc1[:], sc3[:]):
+            nc.scalar.copy(plane.rearrange("p g w -> p (g w)").bitcast(U32),
+                           zero[:, 0:1].bitcast(U32).to_broadcast([P, COLD * S * H // 4]))
         sh2 = hot_planes[:, 0:1, 0 : N // 4]
 
         def scale_rows(plane, row0, dram):
@@ -89,8 +94,8 @@ def tile_moe_hot_glu_sigmoid_kernel(
                 loads += [plane[r] for plane in rows]
         second = [(w2c[e][:].bitcast(I32), w2c_words[e - 1, 0].bitcast(I32)) for e in ORDER[:5]]
         for step in range(1, 5):
-            loads += [cold(w1c, w1c_words, ORDER[step])] + second[step - 2 : step - 1] + [cold(w3c, w3c_words, ORDER[step])]
-        loads += [hot(w1h, w1h_words, 0, S), second[3], hot(w3h, w3h_words, 0, S - 1), second[4], hot(w3h, w3h_words, S - 1, S)]
+            loads += [cold(w1c, w1c_words, ORDER[step]), cold(w3c, w3c_words, ORDER[step])] + second[step - 2 : step - 1]
+        loads += [hot(w1h, w1h_words, 0, S), hot(w3h, w3h_words, 0, S - 1), hot(w3h, w3h_words, S - 1, S)] + second[3:]
         loads += [(w2h[:].bitcast(I32), w2h_words[0, 0].rearrange("p i d -> p (i d)").bitcast(I32))]
         for pair in loads:
             nc.sync.dma_start(*pair)
@@ -138,18 +143,19 @@ def tile_moe_hot_glu_sigmoid_kernel(
             nc.scalar.activation(sg[:], acc, SIGMOID)
             return sg
 
-        def product(step, sg):
-            acc = first_layer(ORDER[step], w3h, w3c, 8, sc3, "b%d" % (step % 2))
-            hid = work.tile([P, 2, P, 2], BF16, name="hid", align_bytes=64)
+        def product(step, acc, sg):
+            hid = keep.tile([P, 2, P, 2], BF16, name="hid" if 1 <= step < E - 1 else "hid%d" % step, align_bytes=64)
             nc.vector.tensor_tensor(hid[:], acc, sg[:], MULT)
             return hid
 
-        def quantise(hid, turned):
+        def turn(hid, turned):
             pairs = hid[:].rearrange("c u p v -> c (u p v)").bitcast(F32)
             for u in range(2):
                 nc.tensor.transpose(turned[:, u, :], pairs[:, u * P : (u + 1) * P], ident[:])
+
+        def quantise(turned):
             grouped = work.tile([P, C * 4], BF16, name="grouped", align_bytes=64)
-            nc.vector.tensor_copy(grouped[:].bitcast(F32).rearrange("p (c u) -> p c u", u=2), turned.rearrange("p u c -> p c u"))
+            nc.scalar.copy(grouped[:].bitcast(F32).rearrange("p (c u) -> p c u", u=2), turned.rearrange("p u c -> p c u"))
             hq = work.tile([P, C], U32, name="hq", align_bytes=64)
             hs = work.tile([P, C], U8, name="hs", align_bytes=64)
             nc.vector.quantize_mx(hq[:].bitcast(FP8X4), hs[:], grouped[:])
@@ -170,28 +176,41 @@ def tile_moe_hot_glu_sigmoid_kernel(
             e = ORDER[step]
             return gate_sb[:, e * C : (e + 1) * C], offsets[:, e * C // 16 : (e + 1) * C // 16]
 
-        def scatter(step, y):
+        def weigh(step, y):
+            gated = work.tile([P, C], F32, name="gated")
+            nc.vector.tensor_tensor(gated[:], y, slots(step)[0], MULT)
+            return gated
+
+        def scatter(step, gated, y):
             weight, listed = slots(step)
-            gated = work.tile([P, 2, C], F32, name="gated")
-            nc.vector.tensor_tensor(gated[:], y, weight.unsqueeze(1).to_broadcast([P, 2, C]), MULT)
-            nc.scalar.activation(windows[0][:].indirect(listed), gated[:, 0, :], COPY)
-            if step < E - 1:
-                nc.scalar.activation(windows[1][:].indirect(listed), gated[:, 1, :], COPY)
-            else:
-                nc.vector.tensor_copy(windows[1][:].indirect(listed), gated[:, 1, :])
+            plain = work.tile([P, C], F32, name="plain")
+            nc.scalar.copy(plain[:], y)
+            nc.scalar.activation(windows[0][:].indirect(listed), gated[:], COPY)
+            nc.vector.tensor_tensor(windows[1][:].indirect(listed), plain[:], weight, MULT)
 
         hids, codes = {}, {}
-        for step in range(E + 2):
-            if step < E:
-                sg = gate_half(step)
+        for step in range(E):
+            sg = gate_half(step)
+            acc = first_layer(ORDER[step], w3h, w3c, 8, sc3, "b%d" % (step % 2))
+            if step == 1:
+                turned = psum.tile([P, 2, C], F32, name="a1")
+                turn(hids[0], turned[:])
+                codes[0] = quantise(turned[:])
             if step >= 2:
-                y = psum.tile([P, 2, C], F32, name="y%d" % (step % 2))
-                second_layer(step - 2, (y[:, 0, :], y[:, 1, :]), *codes[step - 2])
-                scatter(step - 2, y[:])
-            if 1 <= step <= E:
-                turned = psum.tile([P, 2, C], F32, name="a1" if step == 1 else "t%d" % (step % 2))
-                codes[step - 1] = quantise(hids[step - 1], turned[:])
-            if step < E:
-                hids[step] = product(step, sg)
+                shared = psum.tile([P, 4, C], F32, name="y%d" % (step % 2))
+                second_layer(step - 2, (shared[:, 2, :], shared[:, 3, :]), *codes[step - 2])
+                turn(hids[step - 1], shared[:, 0:2, :])
+                gated = weigh(step - 2, shared[:, 2, :])
+            hids[step] = product(step, acc, sg)
+            if step >= 2:
+                codes[step - 1] = quantise(shared[:, 0:2, :])
+                scatter(step - 2, gated, shared[:, 3, :])
+        turned = psum.tile([P, 2, C], F32, name="t0")
+        turn(hids[E - 1], turned[:])
+        codes[E - 1] = quantise(turned[:])
+        for step in (E - 2, E - 1):
+            ys = [psum.tile([P, C], F32, name="%s%d" % (kind, step % 2)) for kind in "ab"]
+            second_layer(step, (ys[0][:], ys[1][:]), *codes[step])
+            scatter(step, weigh(step, ys[0][:]), ys[1][:])
         for h in range(2):
             nc.sync.dma_start(out[h * P : (h + 1) * P, :], windows[h][:])

@@ -45,25 +45,24 @@ def tile_moe_hot_glu_sigmoid_kernel(
         sc3 = keep.tile([P, COLD * S, H // 4], I32, name="sc3", align_bytes=64)
         sc2 = keep.tile([P, COLD, N // 4], I32, name="sc2", align_bytes=64)
         hot_planes = keep.tile([P, S, H // 4], I32, name="hot_planes", align_bytes=64)
+        sh2 = keep.tile([P, 1, N // 4], I32, name="sh2", align_bytes=64)
         gate_rows = keep.tile([P, P], F32, name="gate_rows")
         ident = keep.tile([P, P], F32, name="ident")
         nc.gpsimd.memset(gate_rows[:], 0.0)
         make_identity(nc, ident[:])
         zero = keep.tile([P, 8], I32, name="zero")
         nc.vector.memset(zero[:], 0)
-        for plane in (xs_in[:], hot_planes[:], sc2[:]):
+        for plane in (xs_in[:], hot_planes[:], sc2[:], sh2[:]):
             nc.vector.memset(plane.rearrange("p g w -> p (g w)"), 0)
         for plane in (sc1[:], sc3[:]):
             nc.scalar.copy(plane.rearrange("p g w -> p (g w)").bitcast(U32),
                            zero[:, 0:1].bitcast(U32).to_broadcast([P, COLD * S * H // 4]))
-        sh2 = hot_planes[:, 0:1, 0 : N // 4]
 
         def scale_rows(plane, row0, dram):
             rows = dram.bitcast(I32).rearrange("g (q r) w -> r q g w", r=4)
             return [(plane[row0 + r : P : 32], rows[r]) for r in range(4)]
 
-        first = [keep.tile([P, 2 * H], U8, name="first%d" % s, align_bytes=64) for s in range(S)]
-        w1c = {e: keep.tile([P, S, 2 * H], U8, name="w1_%d" % e, align_bytes=64) for e in ORDER[1:5]}
+        w1c = {e: keep.tile([P, S, 2 * H], U8, name="w1_%d" % e, align_bytes=64) for e in ORDER[:5]}
         w3c = {e: keep.tile([P, S, 2 * H], U8, name="w3_%d" % e, align_bytes=64) for e in ORDER[:5]}
         w2c = {e: keep.tile([P, 2 * N], U8, name="w2_%d" % e, align_bytes=64) for e in ORDER[:5]}
         w1h = keep.tile([P, S, 4 * H], U8, name="w1h", align_bytes=64)
@@ -83,13 +82,11 @@ def tile_moe_hot_glu_sigmoid_kernel(
         r_c2 = scale_rows(sc2[:], 0, w2c_scales.rearrange("f s b i -> (f s) b i"))
         r_h1 = scale_rows(hot_planes[:], 4, w1h_scales[0])
         r_h3 = scale_rows(hot_planes[:], 8, w3h_scales[0])
-        r_h2 = scale_rows(sh2, 12, w2h_scales[0])
-        loads = [(xw_in[s][:], x_words[s].rearrange("p t d -> p (t d)").bitcast(I32)) for s in range(S)]
-        loads = loads[:1] + [(gate_rows[0:ROWS, 0:RUN], gate[0].rearrange("(r c) -> r c", r=ROWS))] + loads[1:]
-        loads += [(first[s][:].bitcast(I32), w1c_words[ORDER[0] - 1, s].bitcast(I32)) for s in range(S)]
-        loads += [cold(w3c, w3c_words, ORDER[0])]
-        loads += r_xs
-        for rows in ((r_c1, r_h1, r_h2), (r_c3, r_h3, r_c2)):
+        r_h2 = scale_rows(sh2[:], 12, w2h_scales[0])
+        tokens = [(xw_in[s][:], x_words[s].rearrange("p t d -> p (t d)").bitcast(I32)) for s in range(S)]
+        loads = tokens[:1] + [(gate_rows[0:ROWS, 0:RUN], gate[0].rearrange("(r c) -> r c", r=ROWS))] + tokens[1:]
+        loads += [cold(w1c, w1c_words, ORDER[0]), cold(w3c, w3c_words, ORDER[0])] + r_xs
+        for rows in ((r_c1, r_h1), (r_c3, r_h3, r_c2)):
             for r in range(4):
                 loads += [plane[r] for plane in rows]
         second = [(w2c[e][:].bitcast(I32), w2c_words[e - 1, 0].bitcast(I32)) for e in ORDER[:5]]
@@ -97,6 +94,7 @@ def tile_moe_hot_glu_sigmoid_kernel(
             loads += [cold(w1c, w1c_words, ORDER[step]), cold(w3c, w3c_words, ORDER[step])] + second[step - 2 : step - 1]
         loads += [hot(w1h, w1h_words, 0, S), hot(w3h, w3h_words, 0, S - 1), hot(w3h, w3h_words, S - 1, S)] + second[3:]
         loads += [(w2h[:].bitcast(I32), w2h_words[0, 0].rearrange("p i d -> p (i d)").bitcast(I32))]
+        loads += r_h2
         for pair in loads:
             nc.sync.dma_start(*pair)
 
@@ -120,7 +118,6 @@ def tile_moe_hot_glu_sigmoid_kernel(
 
         for g in (1, 0):
             gather(words, g, U32, "xw_%d" % g, [xw_in[s][:] for s in range(S)])
-        for g in (1, 0):
             gather(scales, g, U8, "xs_%d" % g, [xs_in[:, s, :] for s in range(S)])
 
         windows = [keep.tile([P, T], F32, name="window%d" % h) for h in range(2)]
@@ -132,7 +129,7 @@ def tile_moe_hot_glu_sigmoid_kernel(
                 if e == 0:
                     rhs, rs = wh[:, s, :].bitcast(FP8X4), hot_planes[row0:P, s, :].bitcast(U8)
                 else:
-                    rhs, rs = (wc[e][:, s, :] if e in wc else first[s][:]).bitcast(FP4X4), sc[:, (e - 1) * S + s, :].bitcast(U8)
+                    rhs, rs = wc[e][:, s, :].bitcast(FP4X4), sc[:, (e - 1) * S + s, :].bitcast(U8)
                 nc.tensor.matmul_mx(acc[:], lhsT=words[g, s][:, cols].bitcast(FP8X4), lhsT_scale=scales[g, s][:, cols],
                                     rhs=rhs, rhs_scale=rs, start=(s == 0), stop=(s == S - 1))
             return acc[:].rearrange("c (p u v) -> c u p v", u=2, v=2)

@@ -39,13 +39,13 @@ def tile_moe_hot_glu_sigmoid_kernel(
         offsets = keep.tile([P, T // 16], U16, name="offsets")
         nc.sync.dma_start(offsets[:], offs)
 
-        xw_in = [keep.tile([P, T], I32, name="xw_in%d" % s, align_bytes=64) for s in range(S)]
-        xs_in = keep.tile([P, S, T // 4], I32, name="xs_in", align_bytes=64)
-        sc1 = keep.tile([P, COLD * S, H // 4], I32, name="sc1", align_bytes=64)
-        sc3 = keep.tile([P, COLD * S, H // 4], I32, name="sc3", align_bytes=64)
-        sc2 = keep.tile([P, COLD, N // 4], I32, name="sc2", align_bytes=64)
-        hot_planes = keep.tile([P, S, H // 4], I32, name="hot_planes", align_bytes=64)
-        sh2 = keep.tile([P, 1, N // 4], I32, name="sh2", align_bytes=64)
+        xw_in = [keep.tile([P, T], I32, name="xw_in%d" % s, align_bytes=256) for s in range(S)]
+        xs_in = keep.tile([P, S, T // 4], I32, name="xs_in", align_bytes=256)
+        sc1 = keep.tile([P, COLD * S, H // 4], I32, name="sc1", align_bytes=256)
+        sc3 = keep.tile([P, COLD * S, H // 4], I32, name="sc3", align_bytes=256)
+        sc2 = keep.tile([P, COLD, N // 4], I32, name="sc2", align_bytes=256)
+        hot_planes = keep.tile([P, S, H // 4], I32, name="hot_planes", align_bytes=256)
+        sh2 = keep.tile([P, 1, N // 4], I32, name="sh2", align_bytes=256)
         gate_rows = keep.tile([P, P], F32, name="gate_rows")
         ident = keep.tile([P, P], F32, name="ident")
         nc.gpsimd.memset(gate_rows[:], 0.0)
@@ -62,12 +62,12 @@ def tile_moe_hot_glu_sigmoid_kernel(
             rows = dram.bitcast(I32).rearrange("g (q r) w -> r q g w", r=4)
             return [(plane[row0 + r : P : 32], rows[r]) for r in range(4)]
 
-        w1c = {e: keep.tile([P, S, 2 * H], U8, name="w1_%d" % e, align_bytes=64) for e in ORDER[:5]}
-        w3c = {e: keep.tile([P, S, 2 * H], U8, name="w3_%d" % e, align_bytes=64) for e in ORDER[:5]}
-        w2c = {e: keep.tile([P, 2 * N], U8, name="w2_%d" % e, align_bytes=64) for e in ORDER[:5]}
-        w1h = keep.tile([P, S, 4 * H], U8, name="w1h", align_bytes=64)
-        w3h = keep.tile([P, S, 4 * H], U8, name="w3h", align_bytes=64)
-        w2h = keep.tile([P, 4 * N], U8, name="w2h", align_bytes=64)
+        w1c = {e: keep.tile([P, S, 2 * H], U8, name="w1_%d" % e, align_bytes=256) for e in ORDER[:5]}
+        w3c = {e: keep.tile([P, S, 2 * H], U8, name="w3_%d" % e, align_bytes=256) for e in ORDER[:5]}
+        w2c = {e: keep.tile([P, 2 * N], U8, name="w2_%d" % e, align_bytes=256) for e in ORDER[:5]}
+        w1h = keep.tile([P, S, 4 * H], U8, name="w1h", align_bytes=256)
+        w3h = keep.tile([P, S, 4 * H], U8, name="w3h", align_bytes=256)
+        w2h = keep.tile([P, 4 * N], U8, name="w2h", align_bytes=256)
         gate_sb = keep.tile([P, T], F32, name="gate_sb")
 
         def cold(tiles, dram, e):
@@ -120,7 +120,7 @@ def tile_moe_hot_glu_sigmoid_kernel(
             gather(words, g, U32, "xw_%d" % g, [xw_in[s][:] for s in range(S)])
             gather(scales, g, U8, "xs_%d" % g, [xs_in[:, s, :] for s in range(S)])
 
-        windows = [keep.tile([P, T], F32, name="window%d" % h) for h in range(2)]
+        windows = [keep.tile([P, T], F32, name="window%d" % h, align_bytes=256) for h in range(2)]
 
         def first_layer(e, wh, wc, row0, sc, bank):
             g, cols = e // 3, slice((e % 3) * C, (e % 3 + 1) * C)

@@ -195,9 +195,13 @@ def tile_moe_hot_glu_sigmoid_kernel(
                 codes[0] = quantise(turned[:])
             if step >= 2:
                 shared = psum.tile([P, 4, C], F32, name="y%d" % (step % 2))
-                second_layer(step - 2, (shared[:, 2, :], shared[:, 3, :]), *codes[step - 2])
+                upper = shared[:, 2, :]
+                if step == E - 1:
+                    apart = psum.tile([P, C], F32, name="t1")
+                    upper = apart[:]
+                second_layer(step - 2, (upper, shared[:, 3, :]), *codes[step - 2])
                 turn(hids[step - 1], shared[:, 0:2, :])
-                gated = weigh(step - 2, shared[:, 2, :])
+                gated = weigh(step - 2, upper)
             hids[step] = product(step, acc, sg)
             if step >= 2:
                 codes[step - 1] = quantise(shared[:, 0:2, :])
@@ -209,5 +213,5 @@ def tile_moe_hot_glu_sigmoid_kernel(
             ys = [psum.tile([P, C], F32, name="%s%d" % (kind, step % 2)) for kind in "ab"]
             second_layer(step, (ys[0][:], ys[1][:]), *codes[step])
             scatter(step, weigh(step, ys[0][:]), ys[1][:])
-        for h in range(2):
-            nc.sync.dma_start(out[h * P : (h + 1) * P, :], windows[h][:])
+        nc.scalar.dma_start(out[0:P, :], windows[0][:])
+        nc.sync.dma_start(out[P:N, :], windows[1][:])

@@ -39,35 +39,35 @@ def tile_moe_hot_glu_sigmoid_kernel(
         offsets = keep.tile([P, T // 16], U16, name="offsets")
         nc.sync.dma_start(offsets[:], offs)
 
-        xw_in = [keep.tile([P, T], I32, name="xw_in%d" % s, align_bytes=256) for s in range(S)]
-        xs_in = keep.tile([P, S, T // 4], I32, name="xs_in", align_bytes=256)
-        sc1 = keep.tile([P, COLD * S, H // 4], I32, name="sc1", align_bytes=256)
-        sc3 = keep.tile([P, COLD * S, H // 4], I32, name="sc3", align_bytes=256)
-        sc2 = keep.tile([P, COLD, N // 4], I32, name="sc2", align_bytes=256)
-        hot_planes = keep.tile([P, S, H // 4], I32, name="hot_planes", align_bytes=256)
-        sh2 = keep.tile([P, 1, N // 4], I32, name="sh2", align_bytes=256)
+        xw_in = [keep.tile([P, T], I32, name="xw_in%d" % s, align_bytes=1024) for s in range(S)]
+        xs_in = keep.tile([P, S, T // 4], I32, name="xs_in", align_bytes=1024)
+        sc1 = keep.tile([P, COLD * S, H // 4], I32, name="sc1", align_bytes=1024)
+        sc3 = keep.tile([P, COLD * S, H // 4], I32, name="sc3", align_bytes=1024)
+        sc2 = keep.tile([P, COLD, N // 4], I32, name="sc2", align_bytes=1024)
+        hot_planes = keep.tile([P, S, H // 4], I32, name="hot_planes", align_bytes=1024)
+        sh2 = keep.tile([P, 1, N // 4], I32, name="sh2", align_bytes=1024)
         gate_rows = keep.tile([P, P], F32, name="gate_rows")
         ident = keep.tile([P, P], F32, name="ident")
         nc.gpsimd.memset(gate_rows[:], 0.0)
         make_identity(nc, ident[:])
-        zero = keep.tile([P, 8], I32, name="zero")
+        zero = keep.tile([P, 1], I32, name="zero")
         nc.vector.memset(zero[:], 0)
         for plane in (xs_in[:], hot_planes[:], sc2[:], sh2[:]):
             nc.vector.memset(plane.rearrange("p g w -> p (g w)"), 0)
         for plane in (sc1[:], sc3[:]):
             nc.scalar.copy(plane.rearrange("p g w -> p (g w)").bitcast(U32),
-                           zero[:, 0:1].bitcast(U32).to_broadcast([P, COLD * S * H // 4]))
+                           zero[:].bitcast(U32).to_broadcast([P, COLD * S * H // 4]))
 
         def scale_rows(plane, row0, dram):
             rows = dram.bitcast(I32).rearrange("g (q r) w -> r q g w", r=4)
             return [(plane[row0 + r : P : 32], rows[r]) for r in range(4)]
 
-        w1c = {e: keep.tile([P, S, 2 * H], U8, name="w1_%d" % e, align_bytes=256) for e in ORDER[:5]}
-        w3c = {e: keep.tile([P, S, 2 * H], U8, name="w3_%d" % e, align_bytes=256) for e in ORDER[:5]}
-        w2c = {e: keep.tile([P, 2 * N], U8, name="w2_%d" % e, align_bytes=256) for e in ORDER[:5]}
-        w1h = keep.tile([P, S, 4 * H], U8, name="w1h", align_bytes=256)
-        w3h = keep.tile([P, S, 4 * H], U8, name="w3h", align_bytes=256)
-        w2h = keep.tile([P, 4 * N], U8, name="w2h", align_bytes=256)
+        w1c = {e: keep.tile([P, S, 2 * H], U8, name="w1_%d" % e, align_bytes=1024) for e in ORDER[:5]}
+        w3c = {e: keep.tile([P, S, 2 * H], U8, name="w3_%d" % e, align_bytes=1024) for e in ORDER[:5]}
+        w2c = {e: keep.tile([P, 2 * N], U8, name="w2_%d" % e, align_bytes=1024) for e in ORDER[:5]}
+        w1h = keep.tile([P, S, 4 * H], U8, name="w1h", align_bytes=1024)
+        w3h = keep.tile([P, S, 4 * H], U8, name="w3h", align_bytes=1024)
+        w2h = keep.tile([P, 4 * N], U8, name="w2h", align_bytes=1024)
         gate_sb = keep.tile([P, T], F32, name="gate_sb")
 
         def cold(tiles, dram, e):
@@ -120,7 +120,7 @@ def tile_moe_hot_glu_sigmoid_kernel(
             gather(words, g, U32, "xw_%d" % g, [xw_in[s][:] for s in range(S)])
             gather(scales, g, U8, "xs_%d" % g, [xs_in[:, s, :] for s in range(S)])
 
-        windows = [keep.tile([P, T], F32, name="window%d" % h, align_bytes=256) for h in range(2)]
+        windows = [keep.tile([P, T], F32, name="window%d" % h, align_bytes=1024) for h in range(2)]
 
         def first_layer(e, wh, wc, row0, sc, bank):
             g, cols = e // 3, slice((e % 3) * C, (e % 3 + 1) * C)

from contextlib import ExitStack

import concourse.mybir as mybir
from concourse.masks import make_identity

K, T, E, C, H, N = 1536, 768, 6, 128, 512, 256
FLOPS = 2 * E * C * (2 * K * H + H * N)

F32 = mybir.dt.float32
BF16 = mybir.dt.bfloat16
I32 = mybir.dt.int32
U32 = mybir.dt.uint32
U16 = mybir.dt.uint16
U8 = mybir.dt.uint8
FP8X4 = mybir.dt.float8_e4m3fn_x4
FP4X4 = mybir.dt.float4_e2m1fn_x4
MULT = mybir.AluOpType.mult
SIGMOID = mybir.ActivationFunctionType.Sigmoid
COPY = mybir.ActivationFunctionType.Copy

P = 128
S = K // 512
COLD = E - 1
ROWS, RUN = 8, T // 8
GROUP = 3 * C
ORDER = [3, 4, 5, 1, 2, 0]


def tile_moe_hot_glu_sigmoid_kernel(
    tc, x_words, x_scales, w1h_words, w1h_scales, w3h_words, w3h_scales, w2h_words, w2h_scales,
    w1c_words, w1c_scales, w3c_words, w3c_scales, w2c_words, w2c_scales, gate, offs, out,
):
    nc = tc.nc
    with ExitStack() as ctx:
        keep = ctx.enter_context(tc.tile_pool(name="keep", bufs=1))
        work = ctx.enter_context(tc.tile_pool(name="work", bufs=3))
        psum = ctx.enter_context(tc.psum_pool(name="psum", bufs=1))

        offsets = keep.tile([P, T // 16], U16, name="offsets")
        nc.sync.dma_start(offsets[:], offs)

        xw_in = [keep.tile([P, T], I32, name="xw_in%d" % s, align_bytes=1024) for s in range(S)]
        xs_in = keep.tile([P, S, T // 4], I32, name="xs_in", align_bytes=1024)
        sc1 = keep.tile([P, COLD * S, H // 4], I32, name="sc1", align_bytes=1024)
        sc3 = keep.tile([P, COLD * S, H // 4], I32, name="sc3", align_bytes=1024)
        sc2 = keep.tile([P, COLD, N // 4], I32, name="sc2", align_bytes=1024)
        hot_planes = keep.tile([P, S, H // 4], I32, name="hot_planes", align_bytes=1024)
        sh2 = keep.tile([P, 1, N // 4], I32, name="sh2", align_bytes=1024)
        gate_rows = keep.tile([P, P], F32, name="gate_rows")
        ident = keep.tile([P, P], F32, name="ident")
        nc.gpsimd.memset(gate_rows[:], 0.0)
        make_identity(nc, ident[:])
        zero = keep.tile([P, 1], I32, name="zero")
        nc.vector.memset(zero[:], 0)
        for plane in (xs_in[:], hot_planes[:], sc2[:], sh2[:]):
            nc.vector.memset(plane.rearrange("p g w -> p (g w)"), 0)
        for plane in (sc1[:], sc3[:]):
            nc.scalar.copy(plane.rearrange("p g w -> p (g w)").bitcast(U32),
                           zero[:].bitcast(U32).to_broadcast([P, COLD * S * H // 4]))

        def scale_rows(plane, row0, dram):
            rows = dram.bitcast(I32).rearrange("g (q r) w -> r q g w", r=4)
            return [(plane[row0 + r : P : 32], rows[r]) for r in range(4)]

        w1c = {e: keep.tile([P, S, 2 * H], U8, name="w1_%d" % e, align_bytes=1024) for e in ORDER[:5]}
        w3c = {e: keep.tile([P, S, 2 * H], U8, name="w3_%d" % e, align_bytes=1024) for e in ORDER[:5]}
        w2c = {e: keep.tile([P, 2 * N], U8, name="w2_%d" % e, align_bytes=1024) for e in ORDER[:5]}
        w1h = keep.tile([P, S, 4 * H], U8, name="w1h", align_bytes=1024)
        w3h = keep.tile([P, S, 4 * H], U8, name="w3h", align_bytes=1024)
        w2h = keep.tile([P, 4 * N], U8, name="w2h", align_bytes=1024)
        gate_sb = keep.tile([P, T], F32, name="gate_sb")

        def cold(tiles, dram, e):
            return (tiles[e][:].bitcast(I32), dram[e - 1].bitcast(I32).rearrange("s p w -> p s w"))

        def hot(tile, dram, a, b):
            return (tile[:, a:b, :].bitcast(I32), dram[0, a:b].rearrange("s p i d -> p s (i d)").bitcast(I32))

        r_xs = scale_rows(xs_in[:], 0, x_scales)
        r_c1 = scale_rows(sc1[:], 0, w1c_scales.rearrange("f s b i -> (f s) b i"))
        r_c3 = scale_rows(sc3[:], 0, w3c_scales.rearrange("f s b i -> (f s) b i"))
        r_c2 = scale_rows(sc2[:], 0, w2c_scales.rearrange("f s b i -> (f s) b i"))
        r_h1 = scale_rows(hot_planes[:], 4, w1h_scales[0])
        r_h3 = scale_rows(hot_planes[:], 8, w3h_scales[0])
        r_h2 = scale_rows(sh2[:], 12, w2h_scales[0])
        tokens = [(xw_in[s][:], x_words[s].rearrange("p t d -> p (t d)").bitcast(I32)) for s in range(S)]
        loads = tokens[:1] + [(gate_rows[0:ROWS, 0:RUN], gate[0].rearrange("(r c) -> r c", r=ROWS))] + tokens[1:]
        loads += [cold(w1c, w1c_words, ORDER[0]), cold(w3c, w3c_words, ORDER[0])] + r_xs
        for rows in ((r_c1, r_h1), (r_c3, r_h3, r_c2)):
            for r in range(4):
                loads += [plane[r] for plane in rows]
        second = [(w2c[e][:].bitcast(I32), w2c_words[e - 1, 0].bitcast(I32)) for e in ORDER[:5]]
        for step in range(1, 5):
            loads += [cold(w1c, w1c_words, ORDER[step]), cold(w3c, w3c_words, ORDER[step])] + second[step - 2 : step - 1]
        loads += [hot(w1h, w1h_words, 0, S), hot(w3h, w3h_words, 0, S - 1), hot(w3h, w3h_words, S - 1, S)] + second[3:]
        loads += [(w2h[:].bitcast(I32), w2h_words[0, 0].rearrange("p i d -> p (i d)").bitcast(I32))]
        loads += r_h2
        for pair in loads:
            nc.sync.dma_start(*pair)

        turned_gate = psum.tile([P, P], F32, name="t0")
        nc.tensor.transpose(turned_gate[:], gate_rows[:], ident[:])
        gate_cols = keep.tile([P, ROWS], F32, name="gate_cols")
        nc.scalar.copy(gate_cols[:], turned_gate[:, 0:ROWS])
        for k in range(2):
            spread = psum.tile([P, 4, P], F32, name="y%d" % k)
            for r in range(4):
                nc.tensor.transpose(spread[:, r, :], gate_cols[:, 4 * k + r : 4 * k + r + 1].to_broadcast([P, P]), ident[:])
            nc.scalar.copy(gate_sb[:, 4 * k * RUN : 4 * (k + 1) * RUN].rearrange("p (r c) -> p r c", r=4), spread[:, :, 0:RUN])

        words, scales = {}, {}

        def gather(found, g, dtype, name, windows_in):
            tile = keep.tile([P, S, GROUP], dtype, name=name, align_bytes=64)
            for s in range(S):
                found[g, s] = tile[:, s, :]
                nc.vector.tensor_copy(found[g, s], windows_in[s].bitcast(dtype).indirect(offsets[:, g * GROUP // 16 : (g + 1) * GROUP // 16]))

        for g in (1, 0):
            gather(words, g, U32, "xw_%d" % g, [xw_in[s][:] for s in range(S)])
            gather(scales, g, U8, "xs_%d" % g, [xs_in[:, s, :] for s in range(S)])

        windows = [keep.tile([P, T], F32, name="window%d" % h, align_bytes=1024) for h in range(2)]

        def first_layer(e, wh, wc, row0, sc, bank):
            g, cols = e // 3, slice((e % 3) * C, (e % 3 + 1) * C)
            acc = psum.tile([P, H], F32, name=bank)
            for s in range(S):
                if e == 0:
                    rhs, rs = wh[:, s, :].bitcast(FP8X4), hot_planes[row0:P, s, :].bitcast(U8)
                else:
                    rhs, rs = wc[e][:, s, :].bitcast(FP4X4), sc[:, (e - 1) * S + s, :].bitcast(U8)
                nc.tensor.matmul_mx(acc[:], lhsT=words[g, s][:, cols].bitcast(FP8X4), lhsT_scale=scales[g, s][:, cols],
                                    rhs=rhs, rhs_scale=rs, start=(s == 0), stop=(s == S - 1))
            return acc[:].rearrange("c (p u v) -> c u p v", u=2, v=2)

        def gate_half(step):
            acc = first_layer(ORDER[step], w1h, w1c, 4, sc1, "a%d" % (step % 2))
            sg = work.tile([P, 2, P, 2], F32, name="sg")
            nc.scalar.activation(sg[:], acc, SIGMOID)
            return sg

        def product(step, acc, sg):
            hid = keep.tile([P, 2, P, 2], BF16, name="hid" if 1 <= step < E - 1 else "hid%d" % step, align_bytes=64)
            nc.vector.tensor_tensor(hid[:], acc, sg[:], MULT)
            return hid

        def turn(hid, turned):
            pairs = hid[:].rearrange("c u p v -> c (u p v)").bitcast(F32)
            for u in range(2):
                nc.tensor.transpose(turned[:, u, :], pairs[:, u * P : (u + 1) * P], ident[:])

        def quantise(turned):
            grouped = work.tile([P, C * 4], BF16, name="grouped", align_bytes=64)
            nc.scalar.copy(grouped[:].bitcast(F32).rearrange("p (c u) -> p c u", u=2), turned.rearrange("p u c -> p c u"))
            hq = work.tile([P, C], U32, name="hq", align_bytes=64)
            hs = work.tile([P, C], U8, name="hs", align_bytes=64)
            nc.vector.quantize_mx(hq[:].bitcast(FP8X4), hs[:], grouped[:])
            return hq, hs

        def second_layer(step, ys, hq, hs):
            e = ORDER[step]
            for h in range(2):
                cols = slice(h * P // 4, (h + 1) * P // 4)
                if e == 0:
                    lhsT, ls = w2h[:, h * 4 * P : (h + 1) * 4 * P].bitcast(FP8X4), sh2[12:P, 0, cols]
                else:
                    lhsT, ls = w2c[e][:, h * 2 * P : (h + 1) * 2 * P].bitcast(FP4X4), sc2[:, e - 1, cols]
                nc.tensor.matmul_mx(ys[h], lhsT=lhsT, lhsT_scale=ls.bitcast(U8), rhs=hq[:].bitcast(FP8X4), rhs_scale=hs[:],
                                    start=True, stop=True)

        def slots(step):
            e = ORDER[step]
            return gate_sb[:, e * C : (e + 1) * C], offsets[:, e * C // 16 : (e + 1) * C // 16]

        def weigh(step, y):
            gated = work.tile([P, C], F32, name="gated")
            nc.vector.tensor_tensor(gated[:], y, slots(step)[0], MULT)
            return gated

        def scatter(step, gated, y):
            weight, listed = slots(step)
            plain = work.tile([P, C], F32, name="plain")
            nc.scalar.copy(plain[:], y)
            nc.scalar.activation(windows[0][:].indirect(listed), gated[:], COPY)
            nc.vector.tensor_tensor(windows[1][:].indirect(listed), plain[:], weight, MULT)

        hids, codes = {}, {}
        for step in range(E):
            sg = gate_half(step)
            acc = first_layer(ORDER[step], w3h, w3c, 8, sc3, "b%d" % (step % 2))
            if step == 1:
                turned = psum.tile([P, 2, C], F32, name="a1")
                turn(hids[0], turned[:])
                codes[0] = quantise(turned[:])
            if step >= 2:
                shared = psum.tile([P, 4, C], F32, name="y%d" % (step % 2))
                upper = shared[:, 2, :]
                if step == E - 1:
                    apart = psum.tile([P, C], F32, name="t1")
                    upper = apart[:]
                second_layer(step - 2, (upper, shared[:, 3, :]), *codes[step - 2])
                turn(hids[step - 1], shared[:, 0:2, :])
                gated = weigh(step - 2, upper)
            hids[step] = product(step, acc, sg)
            if step >= 2:
                codes[step - 1] = quantise(shared[:, 0:2, :])
                scatter(step - 2, gated, shared[:, 3, :])
        turned = psum.tile([P, 2, C], F32, name="t0")
        turn(hids[E - 1], turned[:])
        codes[E - 1] = quantise(turned[:])
        for step in (E - 2, E - 1):
            ys = [psum.tile([P, C], F32, name="%s%d" % (kind, step % 2)) for kind in "ab"]
            second_layer(step, (ys[0][:], ys[1][:]), *codes[step])
            scatter(step, weigh(step, ys[0][:]), ys[1][:])
        nc.scalar.dma_start(out[0:P, :], windows[0][:])
        nc.sync.dma_start(out[P:N, :], windows[1][:])
